import numpy as np
import ml_dtypes


def mxq(x, axis, fmt="e4m3"):
    dtype, down = {"e4m3": (ml_dtypes.float8_e4m3fn, 7), "e5m2": (ml_dtypes.float8_e5m2, 14)}[fmt]
    v = np.moveaxis(np.asarray(x, np.float32).astype(ml_dtypes.bfloat16).astype(np.float64), axis, -1)
    blocks = v.reshape(v.shape[:-1] + (-1, 32))
    amax = np.abs(blocks).max(-1, keepdims=True)
    byte = np.maximum(np.where(amax > 0, np.frexp(amax)[1] - 1 + 127, 0) - down, 1)
    scale = np.exp2(byte - 127.0)
    codes = (blocks / scale).astype(np.float32).astype(dtype).astype(np.float64)
    return np.moveaxis((codes * scale).reshape(v.shape), -1, axis)


WIDE = False


def mx_kscale(k):
    if not WIDE:
        return np.ones(k)
    levels = np.array([10, -10, 5, -5, 0])
    if k % 512:
        return np.exp2(np.random.permutation(np.resize(levels, k // 32))).repeat(32)
    a = np.empty((k // 512, 16))
    for p in range(k // 512):
        a[p, :8] = np.random.permutation(np.resize(levels, 8))
        for g in range(8):
            far = levels[np.abs(levels - a[p, g]) >= 10]
            a[p, g + 8] = far[np.random.randint(len(far))]
    return np.exp2(a.ravel()).repeat(32)


def f64(x):
    return np.asarray(x).astype(np.float64)


def striped(idx):
    return np.tile(idx.reshape(-1, 16).T, (8, 1)).astype(np.uint16)


def unstriped(offs):
    return offs[:16].T.reshape(-1).astype(np.int64)


def pack_weight(w):
    k, n = w.shape
    w = f64(np.asarray(w, np.float32).astype(ml_dtypes.bfloat16)).reshape(k // 32, 32, n)
    amax = np.abs(w).max(1)
    byte = np.clip(np.where(amax > 0, np.frexp(amax)[1] - 1 + 127 - 7, 1), 1, 254)
    scaled = (w * np.exp2(127.0 - byte)[:, None, :]).reshape(k, n).astype(np.float32)
    words = np.ascontiguousarray(scaled.reshape(k // 512, 128, 4, n).transpose(0, 1, 3, 2)).astype(ml_dtypes.float8_e4m3fn).view(np.uint8)
    return words, np.ascontiguousarray(byte.astype(np.uint8).reshape(k // 512, 16, n))


def unpack_weight(words, scales):
    g, p, n, _ = words.shape
    vals = np.ascontiguousarray(words).view(ml_dtypes.float8_e4m3fn).astype(np.float64) * np.repeat(np.exp2(scales.astype(np.float64) - 127.0), 8, axis=1)[..., None]
    return vals.transpose(0, 1, 3, 2).reshape(g * 512, n)


K, T, S, H, D, W, U = 1024, 2048, 512, 512, 2, 2048, 512


def setup_inputs():
    n = np.random.standard_normal
    s = mx_kscale(K)[:, None]
    u = mx_kscale(H)
    packed_xT = pack_weight(n((K, T)) * s)
    packed_eT = pack_weight(n((H, W)) / np.sqrt(H) / u[:, None])
    return {
        "x_words": packed_xT[0],
        "x_scales": packed_xT[1],
        "w1": (n((K, H)) / np.sqrt(K) / s * u).astype(np.float32),
        "e_words": packed_eT[0],
        "e_scales": packed_eT[1],
        "offs": striped(np.random.permutation(T)[:S]),
        "sup": striped(np.random.permutation(W)[:U]),
    }


def reference(x_words, x_scales, w1, e_words, e_scales, offs, sup):
    xq = unpack_weight(x_words, x_scales)[:, unstriped(offs)]
    h = mxq(f64(w1), 0, "e4m3").T @ xq
    e_sup = unpack_weight(e_words, e_scales)[:, unstriped(sup)]
    y = mxq(h, 0, "e4m3").T @ e_sup
    ex = np.exp(y - y.max(axis=1, keepdims=True))
    p = ex / ex.sum(axis=1, keepdims=True)
    return p.reshape(len(p), -1, D).sum(axis=2)

@@ -1,0 +1,176 @@
+from contextlib import ExitStack
+
+import concourse.mybir as mybir
+
+K, T, S, H, D, W, U = 1024, 2048, 512, 512, 2, 2048, 512
+FLOPS = 2 * K * H * S + 2 * H * S * U
+
+F32 = mybir.dt.float32
+BF16 = mybir.dt.bfloat16
+I32 = mybir.dt.int32
+U32 = mybir.dt.uint32
+U16 = mybir.dt.uint16
+U8 = mybir.dt.uint8
+FP8X4 = mybir.dt.float8_e4m3fn_x4
+ALU = mybir.AluOpType
+ACT = mybir.ActivationFunctionType
+
+P = 128
+PACK = 4
+K_PASS = P * PACK
+PASSES = K // K_PASS
+QUADS = 4
+Q_TILE = 128
+Q_TILES = S // Q_TILE
+HALF = S // 2
+E_ROW = 8
+M_SCALAR = 80
+
+
+def tile_picked_ymatch_sum_p_kernel(tc, x_words, x_scales, w1, e_words, e_scales, offs, sup, out):
+    nc = tc.nc
+    with ExitStack() as ctx:
+        lists = ctx.enter_context(tc.tile_pool(name="lists", bufs=1))
+        held = ctx.enter_context(tc.tile_pool(name="held", bufs=1))
+        psum = ctx.enter_context(tc.psum_pool(name="psum", bufs=1))
+
+        offs_sb = lists.tile([P, S // 16], U16, name="offs_sb")
+        sup_sb = lists.tile([P, U // 16], U16, name="sup_sb")
+
+        x_scale_table = held.tile([P, T], U8, name="x_scale_table", tag="reuse1", align_bytes=64)
+        e_scale_table = held.tile([P, W], U8, name="e_scale_table", align_bytes=64)
+        for table in (x_scale_table, e_scale_table):
+            nc.vector.memset(table[:].bitcast(I32), 0)
+
+        w_raw = [held.tile([P, PACK, H], F32, name=f"w_raw{g}") for g in range(PASSES)]
+        x_table = [held.tile([P, T], I32, name=f"x_table{g}", align_bytes=64) for g in range(PASSES)]
+        e_table = held.tile([P, W], I32, name="e_table", tag="e_table_then_h_codes", align_bytes=64)
+
+        def load_w(g):
+            nc.sync.dma_start(out=w_raw[g][:], in_=w1[g * K_PASS : (g + 1) * K_PASS, :].rearrange("(p j) c -> p j c", j=PACK))
+
+        def load_words(table, words):
+            nc.sync.dma_start(out=table[:], in_=words.rearrange("p n j -> p (n j)").bitcast(I32))
+
+        def load_x_scales(q):
+            for g in range(PASSES):
+                nc.sync.dma_start(
+                    out=x_scale_table[32 * q + 4 * g : 32 * q + 4 * g + 4, :].bitcast(I32),
+                    in_=x_scales[g, 4 * q : 4 * q + 4, :].bitcast(I32),
+                )
+
+        load_w(0)
+        nc.sync.dma_start(offs_sb[:], offs)
+        load_x_scales(0)
+        load_x_scales(2)
+        load_w(1)
+        nc.sync.dma_start(sup_sb[:], sup)
+        load_x_scales(1)
+        load_x_scales(3)
+        load_words(x_table[0], x_words[0])
+        for q in (0, 2, 1, 3):
+            nc.sync.dma_start(
+                out=e_scale_table[32 * q + E_ROW : 32 * q + E_ROW + 4, :].bitcast(I32),
+                in_=e_scales[0, 4 * q : 4 * q + 4, :].bitcast(I32),
+            )
+        load_words(x_table[1], x_words[1])
+        load_words(e_table, e_words[0])
+
+        w_codes = []
+        w_scale = [held.tile([P, H], U8, name=f"w_scale{g}", align_bytes=64) for g in range(PASSES)]
+        w_bf = [held.tile([P, PACK, P, PACK], BF16, name=f"w_bf{g}", align_bytes=64) for g in range(PASSES)]
+
+        def round_w(g):
+            dst = w_bf[g][:].rearrange("p t m j -> p m t j")
+            src = w_raw[g][:].rearrange("p j (m t) -> p m t j", t=PACK)
+            nc.scalar.copy(out=dst[:, :M_SCALAR], in_=src[:, :M_SCALAR])
+            nc.vector.tensor_copy(out=dst[:, M_SCALAR:], in_=src[:, M_SCALAR:])
+
+        def quantise_w(g):
+            w_codes.append(held.tile([P, H], U32, name=f"w_codes{g}", tag=f"reuse{g}", align_bytes=64))
+            nc.vector.quantize_mx(out=w_codes[g][:].bitcast(FP8X4), scales=w_scale[g][:], in_=w_bf[g][:].rearrange("p t m j -> p (t m j)"))
+
+        x_scale = held.tile([P, S], U8, name="x_scale", align_bytes=64)
+        e_scale = held.tile([P, U], U8, name="e_scale", align_bytes=64)
+        x_codes = [[held.tile([P, HALF], U32, name=f"x_codes{g}_{u}", align_bytes=64) for u in range(2)] for g in range(PASSES)]
+        e_codes = held.tile([P, U], U32, name="e_codes", align_bytes=64)
+
+        round_w(0)
+        quantise_w(0)
+        round_w(1)
+        nc.vector.tensor_copy(x_scale[:], x_scale_table[:].indirect(offs_sb[:]))
+        quantise_w(1)
+
+        h_ps = [psum.tile([P, PACK, Q_TILE], F32, name=f"h_ps{b}") for b in range(Q_TILES)]
+        y_ps = [psum.tile([P, U], F32, name=f"y_ps{b}") for b in range(Q_TILES)]
+        h_bf = [held.tile([P, Q_TILE, PACK], BF16, name=f"h_bf{b}", align_bytes=64) for b in range(Q_TILES)]
+        h_scale = [held.tile([P, Q_TILE], U8, name=f"h_scale{b}", align_bytes=64) for b in range(Q_TILES)]
+
+        def gather_x(g, u):
+            cols = slice(u * HALF // 16, (u + 1) * HALF // 16)
+            nc.vector.tensor_copy(x_codes[g][u][:], x_table[g][:].bitcast(U32).indirect(offs_sb[:, cols]))
+
+        def project(g, b):
+            u, c = divmod(b * Q_TILE, HALF)
+            for t in range(PACK):
+                nc.tensor.matmul_mx(
+                    out=h_ps[b][:, t, :],
+                    lhsT=w_codes[g][:, t * P : (t + 1) * P].bitcast(FP8X4),
+                    lhsT_scale=w_scale[g][:, t * P : (t + 1) * P],
+                    rhs=x_codes[g][u][:, c : c + Q_TILE].bitcast(FP8X4),
+                    rhs_scale=x_scale[4 * g : P, b * Q_TILE : (b + 1) * Q_TILE],
+                    start=(g == 0 and t == 0),
+                    stop=(g == PASSES - 1 and t == PACK - 1),
+                )
+
+        for u in range(2):
+            gather_x(0, u)
+        for b in range(Q_TILES):
+            project(0, b)
+        nc.vector.tensor_copy(e_scale[:], e_scale_table[:].indirect(sup_sb[:]))
+        for u in range(2):
+            gather_x(1, u)
+        for b in range(Q_TILES):
+            project(1, b)
+
+        def quantise_h(b, codes):
+            nc.vector.quantize_mx(out=codes.bitcast(FP8X4), scales=h_scale[b][:], in_=h_bf[b][:].rearrange("p q t -> p (q t)"))
+
+        for b in range(Q_TILES):
+            nc.scalar.copy(out=h_bf[b][:], in_=h_ps[b][:].rearrange("p t q -> p q t"))
+
+        h_codes_first = held.tile([P, Q_TILE], U32, name="h_codes_first", align_bytes=64)
+        quantise_h(0, h_codes_first[:])
+        nc.vector.tensor_copy(e_codes[:], e_table[:].bitcast(U32).indirect(sup_sb[:]))
+        h_codes_rest = held.tile([P, Q_TILES - 1, Q_TILE], U32, name="h_codes_rest", tag="e_table_then_h_codes", align_bytes=64)
+        h_codes = [h_codes_first[:]] + [h_codes_rest[:, b - 1, :] for b in range(1, Q_TILES)]
+        for b in range(1, Q_TILES):
+            quantise_h(b, h_codes[b])
+
+        for b in range(Q_TILES):
+            nc.tensor.matmul_mx(
+                out=y_ps[b][:],
+                lhsT=h_codes[b].bitcast(FP8X4),
+                lhsT_scale=h_scale[b][:],
+                rhs=e_codes[:].bitcast(FP8X4),
+                rhs_scale=e_scale[E_ROW:P, :],
+                start=True,
+                stop=True,
+            )
+
+        for b in range(Q_TILES):
+            neg_max = held.tile([P, 1], F32, name=f"neg_max{b}")
+            total = held.tile([P, 1], F32, name=f"total{b}")
+            inv = held.tile([P, 1], F32, name=f"inv{b}")
+            ex = held.tile([P, D, U // D], F32, name=f"ex{b}")
+            pair = held.tile([P, U // D], F32, name=f"pair{b}")
+            prob = held.tile([P, U // D], F32, name=f"prob{b}")
+            nc.vector.tensor_reduce(out=neg_max[:], in_=y_ps[b][:], axis=mybir.AxisListType.X, op=ALU.max, negate=True)
+            nc.scalar.activation(out=ex[:], in_=y_ps[b][:].rearrange("p (v d) -> p d v", d=D), func=ACT.Exp, bias=neg_max[:], scale=1.0, accum_out=total[:])
+            nc.vector.reciprocal(out=inv[:], in_=total[:])
+            nc.vector.tensor_tensor(out=pair[:], in0=ex[:, 0, :], in1=ex[:, 1, :], op=ALU.add)
+            if b < Q_TILES - 1:
+                nc.scalar.activation(out=prob[:], in_=pair[:], func=ACT.Copy, scale=inv[:])
+            else:
+                nc.vector.tensor_scalar(out=prob[:], in0=pair[:], scalar1=inv[:], scalar2=None, op0=ALU.mult)
+            nc.sync.dma_start(out=out[b * Q_TILE : (b + 1) * Q_TILE, :], in_=prob[:])

@@ -24,7 +24,7 @@ Q_TILE = 128
 Q_TILES = S // Q_TILE
 HALF = S // 2
 E_ROW = 8
-M_SCALAR = 80
+M_SCALAR = 88
 
 
 def tile_picked_ymatch_sum_p_kernel(tc, x_words, x_scales, w1, e_words, e_scales, offs, sup, out):
@@ -37,13 +37,13 @@ def tile_picked_ymatch_sum_p_kernel(tc, x_words, x_scales, w1, e_words, e_scales
         offs_sb = lists.tile([P, S // 16], U16, name="offs_sb")
         sup_sb = lists.tile([P, U // 16], U16, name="sup_sb")
 
-        x_scale_table = held.tile([P, T], U8, name="x_scale_table", tag="reuse1", align_bytes=64)
-        e_scale_table = held.tile([P, W], U8, name="e_scale_table", align_bytes=64)
-        for table in (x_scale_table, e_scale_table):
-            nc.vector.memset(table[:].bitcast(I32), 0)
+        x_scale_table = held.tile([P, T], U8, name="x_scale_table", align_bytes=64)
+        e_scale_table = held.tile([P, W], U8, name="e_scale_table", tag="e_scale_table", align_bytes=64)
+        nc.gpsimd.memset(x_scale_table[:].bitcast(I32), 0)
+        nc.vector.memset(e_scale_table[:].bitcast(I32), 0)
 
         w_raw = [held.tile([P, PACK, H], F32, name=f"w_raw{g}") for g in range(PASSES)]
-        x_table = [held.tile([P, T], I32, name=f"x_table{g}", align_bytes=64) for g in range(PASSES)]
+        x_table = [held.tile([P, T], I32, name=f"x_table{g}", tag=f"x_table{g}", align_bytes=64) for g in range(PASSES)]
         e_table = held.tile([P, W], I32, name="e_table", tag="e_table_then_h_codes", align_bytes=64)
 
         def load_w(g):
@@ -52,59 +52,48 @@ def tile_picked_ymatch_sum_p_kernel(tc, x_words, x_scales, w1, e_words, e_scales
         def load_words(table, words):
             nc.sync.dma_start(out=table[:], in_=words.rearrange("p n j -> p (n j)").bitcast(I32))
 
-        def load_x_scales(q):
-            for g in range(PASSES):
-                nc.sync.dma_start(
-                    out=x_scale_table[32 * q + 4 * g : 32 * q + 4 * g + 4, :].bitcast(I32),
-                    in_=x_scales[g, 4 * q : 4 * q + 4, :].bitcast(I32),
-                )
-
+        for q in (0, 2, 1, 3):
+            nc.gpsimd.dma_start(
+                out=x_scale_table[32 * q : 32 * q + 4 * PASSES, :].bitcast(I32),
+                in_=x_scales[:, 4 * q : 4 * q + 4, :].bitcast(I32),
+            )
         load_w(0)
         nc.sync.dma_start(offs_sb[:], offs)
-        load_x_scales(0)
-        load_x_scales(2)
-        load_w(1)
         nc.sync.dma_start(sup_sb[:], sup)
-        load_x_scales(1)
-        load_x_scales(3)
-        load_words(x_table[0], x_words[0])
-        for q in (0, 2, 1, 3):
+        for r in range(4):
             nc.sync.dma_start(
-                out=e_scale_table[32 * q + E_ROW : 32 * q + E_ROW + 4, :].bitcast(I32),
-                in_=e_scales[0, 4 * q : 4 * q + 4, :].bitcast(I32),
+                out=e_scale_table[E_ROW + r : P : 32, :].bitcast(I32),
+                in_=e_scales[0, r:16:4, :].bitcast(I32),
             )
+        load_w(1)
+        load_words(x_table[0], x_words[0])
         load_words(x_table[1], x_words[1])
         load_words(e_table, e_words[0])
 
         w_codes = []
         w_scale = [held.tile([P, H], U8, name=f"w_scale{g}", align_bytes=64) for g in range(PASSES)]
-        w_bf = [held.tile([P, PACK, P, PACK], BF16, name=f"w_bf{g}", align_bytes=64) for g in range(PASSES)]
+        w_bf = [held.tile([P, PACK, P, PACK], BF16, name=f"w_bf{g}", tag=f"w_bf{g}", align_bytes=64) for g in range(PASSES)]
 
-        def round_w(g):
+        def round_w(g, m_scalar):
             dst = w_bf[g][:].rearrange("p t m j -> p m t j")
             src = w_raw[g][:].rearrange("p j (m t) -> p m t j", t=PACK)
-            nc.scalar.copy(out=dst[:, :M_SCALAR], in_=src[:, :M_SCALAR])
-            nc.vector.tensor_copy(out=dst[:, M_SCALAR:], in_=src[:, M_SCALAR:])
+            nc.scalar.copy(out=dst[:, :m_scalar], in_=src[:, :m_scalar])
+            if m_scalar < P:
+                nc.vector.tensor_copy(out=dst[:, m_scalar:], in_=src[:, m_scalar:])
 
-        def quantise_w(g):
-            w_codes.append(held.tile([P, H], U32, name=f"w_codes{g}", tag=f"reuse{g}", align_bytes=64))
+        def quantise_w(g, tag):
+            w_codes.append(held.tile([P, H], U32, name=f"w_codes{g}", tag=tag, align_bytes=64))
             nc.vector.quantize_mx(out=w_codes[g][:].bitcast(FP8X4), scales=w_scale[g][:], in_=w_bf[g][:].rearrange("p t m j -> p (t m j)"))
 
-        x_scale = held.tile([P, S], U8, name="x_scale", align_bytes=64)
         e_scale = held.tile([P, U], U8, name="e_scale", align_bytes=64)
         x_codes = [[held.tile([P, HALF], U32, name=f"x_codes{g}_{u}", align_bytes=64) for u in range(2)] for g in range(PASSES)]
         e_codes = held.tile([P, U], U32, name="e_codes", align_bytes=64)
 
-        round_w(0)
-        quantise_w(0)
-        round_w(1)
-        nc.vector.tensor_copy(x_scale[:], x_scale_table[:].indirect(offs_sb[:]))
-        quantise_w(1)
 
         h_ps = [psum.tile([P, PACK, Q_TILE], F32, name=f"h_ps{b}") for b in range(Q_TILES)]
         y_ps = [psum.tile([P, U], F32, name=f"y_ps{b}") for b in range(Q_TILES)]
-        h_bf = [held.tile([P, Q_TILE, PACK], BF16, name=f"h_bf{b}", align_bytes=64) for b in range(Q_TILES)]
-        h_scale = [held.tile([P, Q_TILE], U8, name=f"h_scale{b}", align_bytes=64) for b in range(Q_TILES)]
+        h_bf = held.tile([P, Q_TILES, Q_TILE, PACK], BF16, name="h_bf", align_bytes=64)
+        h_scale = held.tile([P, S], U8, name="h_scale", align_bytes=64)
 
         def gather_x(g, u):
             cols = slice(u * HALF // 16, (u + 1) * HALF // 16)
@@ -123,35 +112,41 @@ def tile_picked_ymatch_sum_p_kernel(tc, x_words, x_scales, w1, e_words, e_scales
                     stop=(g == PASSES - 1 and t == PACK - 1),
                 )
 
+        round_w(0, M_SCALAR)
+        nc.vector.tensor_copy(e_scale[:], e_scale_table[:].indirect(sup_sb[:]))
+        quantise_w(0, "e_scale_table")
+        x_scale = held.tile([P, S], U8, name="x_scale", tag="w_bf0", align_bytes=64)
+        nc.vector.tensor_copy(x_scale[:], x_scale_table[:].indirect(offs_sb[:]))
+        round_w(1, P)
         for u in range(2):
             gather_x(0, u)
         for b in range(Q_TILES):
             project(0, b)
-        nc.vector.tensor_copy(e_scale[:], e_scale_table[:].indirect(sup_sb[:]))
+        quantise_w(1, "x_table0")
         for u in range(2):
             gather_x(1, u)
         for b in range(Q_TILES):
             project(1, b)
 
-        def quantise_h(b, codes):
-            nc.vector.quantize_mx(out=codes.bitcast(FP8X4), scales=h_scale[b][:], in_=h_bf[b][:].rearrange("p q t -> p (q t)"))
+        def quantise_h(codes, scales, lo, hi):
+            nc.vector.quantize_mx(out=codes.bitcast(FP8X4), scales=scales, in_=h_bf[:, lo:hi].rearrange("p b q t -> p (b q t)"))
 
         for b in range(Q_TILES):
-            nc.scalar.copy(out=h_bf[b][:], in_=h_ps[b][:].rearrange("p t q -> p q t"))
+            nc.scalar.copy(out=h_bf[:, b], in_=h_ps[b][:].rearrange("p t q -> p q t"))
 
         h_codes_first = held.tile([P, Q_TILE], U32, name="h_codes_first", align_bytes=64)
-        quantise_h(0, h_codes_first[:])
+        quantise_h(h_codes_first[:], h_scale[:, :Q_TILE], 0, 1)
         nc.vector.tensor_copy(e_codes[:], e_table[:].bitcast(U32).indirect(sup_sb[:]))
-        h_codes_rest = held.tile([P, Q_TILES - 1, Q_TILE], U32, name="h_codes_rest", tag="e_table_then_h_codes", align_bytes=64)
-        h_codes = [h_codes_first[:]] + [h_codes_rest[:, b - 1, :] for b in range(1, Q_TILES)]
-        for b in range(1, Q_TILES):
-            quantise_h(b, h_codes[b])
+        h_codes_rest = held.tile([P, S - Q_TILE], U32, name="h_codes_rest", tag="e_table_then_h_codes", align_bytes=64)
+        quantise_h(h_codes_rest[:, :Q_TILE], h_scale[:, Q_TILE:HALF], 1, 2)
+        quantise_h(h_codes_rest[:, Q_TILE:], h_scale[:, HALF:], 2, 4)
+        h_codes = [h_codes_first[:]] + [h_codes_rest[:, (b - 1) * Q_TILE : b * Q_TILE] for b in range(1, Q_TILES)]
 
         for b in range(Q_TILES):
             nc.tensor.matmul_mx(
                 out=y_ps[b][:],
                 lhsT=h_codes[b].bitcast(FP8X4),
-                lhsT_scale=h_scale[b][:],
+                lhsT_scale=h_scale[:, b * Q_TILE : (b + 1) * Q_TILE],
                 rhs=e_codes[:].bitcast(FP8X4),
                 rhs_scale=e_scale[E_ROW:P, :],
                 start=True,

@@ -23,7 +23,6 @@ QUADS = 4
 Q_TILE = 128
 Q_TILES = S // Q_TILE
 HALF = S // 2
-E_ROW = 8
 M_SCALAR = 88
 
 
@@ -41,6 +40,10 @@ def tile_picked_ymatch_sum_p_kernel(tc, x_words, x_scales, w1, e_words, e_scales
         e_scale_table = held.tile([P, W], U8, name="e_scale_table", tag="e_scale_table", align_bytes=64)
         nc.gpsimd.memset(x_scale_table[:].bitcast(I32), 0)
         nc.vector.memset(e_scale_table[:].bitcast(I32), 0)
+        x_scale = held.tile([P, S], U8, name="x_scale", align_bytes=64)
+        e_scale = held.tile([P, U], U8, name="e_scale", align_bytes=64)
+        nc.vector.memset(x_scale[:].bitcast(I32), 0)
+        nc.vector.memset(e_scale[:].bitcast(I32), 0)
 
         w_raw = [held.tile([P, PACK, H], F32, name=f"w_raw{g}") for g in range(PASSES)]
         x_table = [held.tile([P, T], I32, name=f"x_table{g}", tag=f"x_table{g}", align_bytes=64) for g in range(PASSES)]
@@ -52,27 +55,21 @@ def tile_picked_ymatch_sum_p_kernel(tc, x_words, x_scales, w1, e_words, e_scales
         def load_words(table, words):
             nc.sync.dma_start(out=table[:], in_=words.rearrange("p n j -> p (n j)").bitcast(I32))
 
-        for q in (0, 2, 1, 3):
-            nc.gpsimd.dma_start(
-                out=x_scale_table[32 * q : 32 * q + 4 * PASSES, :].bitcast(I32),
-                in_=x_scales[:, 4 * q : 4 * q + 4, :].bitcast(I32),
-            )
         load_w(0)
         nc.sync.dma_start(offs_sb[:], offs)
-        nc.sync.dma_start(sup_sb[:], sup)
-        for r in range(4):
+        for g in range(PASSES):
             nc.sync.dma_start(
-                out=e_scale_table[E_ROW + r : P : 32, :].bitcast(I32),
-                in_=e_scales[0, r:16:4, :].bitcast(I32),
+                out=x_scale_table[64 * g : 64 * (g + 1) : 4, :].bitcast(I32),
+                in_=x_scales[g].rearrange("(q r) c -> r q c", r=4).bitcast(I32),
             )
+        nc.sync.dma_start(sup_sb[:], sup)
+        nc.sync.dma_start(out=e_scale_table[0:P:8, :].bitcast(I32), in_=e_scales[0].bitcast(I32))
         load_w(1)
         load_words(x_table[0], x_words[0])
-        load_words(x_table[1], x_words[1])
-        load_words(e_table, e_words[0])
 
         w_codes = []
         w_scale = [held.tile([P, H], U8, name=f"w_scale{g}", align_bytes=64) for g in range(PASSES)]
-        w_bf = [held.tile([P, PACK, P, PACK], BF16, name=f"w_bf{g}", tag=f"w_bf{g}", align_bytes=64) for g in range(PASSES)]
+        w_bf = [held.tile([P, PACK, P, PACK], BF16, name=f"w_bf{g}", align_bytes=64) for g in range(PASSES)]
 
         def round_w(g, m_scalar):
             dst = w_bf[g][:].rearrange("p t m j -> p m t j")
@@ -85,7 +82,8 @@ def tile_picked_ymatch_sum_p_kernel(tc, x_words, x_scales, w1, e_words, e_scales
             w_codes.append(held.tile([P, H], U32, name=f"w_codes{g}", tag=tag, align_bytes=64))
             nc.vector.quantize_mx(out=w_codes[g][:].bitcast(FP8X4), scales=w_scale[g][:], in_=w_bf[g][:].rearrange("p t m j -> p (t m j)"))
 
-        e_scale = held.tile([P, U], U8, name="e_scale", align_bytes=64)
+        x_scale_picked = held.tile([P, S], U8, name="x_scale_picked", align_bytes=64)
+        e_scale_picked = held.tile([P, U], U8, name="e_scale_picked", align_bytes=64)
         x_codes = [[held.tile([P, HALF], U32, name=f"x_codes{g}_{u}", align_bytes=64) for u in range(2)] for g in range(PASSES)]
         e_codes = held.tile([P, U], U32, name="e_codes", align_bytes=64)
 
@@ -113,10 +111,15 @@ def tile_picked_ymatch_sum_p_kernel(tc, x_words, x_scales, w1, e_words, e_scales
                 )
 
         round_w(0, M_SCALAR)
-        nc.vector.tensor_copy(e_scale[:], e_scale_table[:].indirect(sup_sb[:]))
+        nc.vector.tensor_copy(x_scale_picked[:], x_scale_table[:].indirect(offs_sb[:]))
+        for q in range(QUADS):
+            nc.sync.dma_start(out=x_scale[32 * q : 32 * q + 8, :].bitcast(I32), in_=x_scale_picked[4 * q : P : 16, :].bitcast(I32))
+        load_words(x_table[1], x_words[1])
+        load_words(e_table, e_words[0])
+        nc.vector.tensor_copy(e_scale_picked[:], e_scale_table[:].indirect(sup_sb[:]))
+        for r in range(4):
+            nc.sync.dma_start(out=e_scale[r:P:32, :].bitcast(I32), in_=e_scale_picked[8 * r : P : 32, :].bitcast(I32))
         quantise_w(0, "e_scale_table")
-        x_scale = held.tile([P, S], U8, name="x_scale", tag="w_bf0", align_bytes=64)
-        nc.vector.tensor_copy(x_scale[:], x_scale_table[:].indirect(offs_sb[:]))
         round_w(1, P)
         for u in range(2):
             gather_x(0, u)
@@ -148,7 +151,7 @@ def tile_picked_ymatch_sum_p_kernel(tc, x_words, x_scales, w1, e_words, e_scales
                 lhsT=h_codes[b].bitcast(FP8X4),
                 lhsT_scale=h_scale[:, b * Q_TILE : (b + 1) * Q_TILE],
                 rhs=e_codes[:].bitcast(FP8X4),
-                rhs_scale=e_scale[E_ROW:P, :],
+                rhs_scale=e_scale[:],
                 start=True,
                 stop=True,
             )

@@ -20,10 +20,13 @@ PACK = 4
 K_PASS = P * PACK
 PASSES = K // K_PASS
 QUADS = 4
+QUAD_ROWS = 4
+LIST_ROWS = 16
 Q_TILE = 128
 Q_TILES = S // Q_TILE
 HALF = S // 2
-M_SCALAR = 88
+CLASSES = U // D
+SCALAR_GROUPS_PASS0 = 88
 
 
 def tile_picked_ymatch_sum_p_kernel(tc, x_words, x_scales, w1, e_words, e_scales, offs, sup, out):
@@ -33,11 +36,11 @@ def tile_picked_ymatch_sum_p_kernel(tc, x_words, x_scales, w1, e_words, e_scales
         held = ctx.enter_context(tc.tile_pool(name="held", bufs=1))
         psum = ctx.enter_context(tc.psum_pool(name="psum", bufs=1))
 
-        offs_sb = lists.tile([P, S // 16], U16, name="offs_sb")
-        sup_sb = lists.tile([P, U // 16], U16, name="sup_sb")
+        offs_sb = lists.tile([P, S // LIST_ROWS], U16, name="offs_sb")
+        sup_sb = lists.tile([P, U // LIST_ROWS], U16, name="sup_sb")
 
         x_scale_table = held.tile([P, T], U8, name="x_scale_table", align_bytes=64)
-        e_scale_table = held.tile([P, W], U8, name="e_scale_table", tag="e_scale_table", align_bytes=64)
+        e_scale_table = held.tile([P, W], U8, name="e_scale_table", tag="e_scale_table_then_w_codes0", align_bytes=64)
         nc.gpsimd.memset(x_scale_table[:].bitcast(I32), 0)
         nc.vector.memset(e_scale_table[:].bitcast(I32), 0)
         x_scale = held.tile([P, S], U8, name="x_scale", align_bytes=64)
@@ -46,8 +49,9 @@ def tile_picked_ymatch_sum_p_kernel(tc, x_words, x_scales, w1, e_words, e_scales
         nc.vector.memset(e_scale[:].bitcast(I32), 0)
 
         w_raw = [held.tile([P, PACK, H], F32, name=f"w_raw{g}") for g in range(PASSES)]
-        x_table = [held.tile([P, T], I32, name=f"x_table{g}", tag=f"x_table{g}", align_bytes=64) for g in range(PASSES)]
-        e_table = held.tile([P, W], I32, name="e_table", tag="e_table_then_h_codes", align_bytes=64)
+        x_table_tags = ("x_table0_then_w_codes1", "x_table1")
+        x_table = [held.tile([P, T], I32, name=f"x_table{g}", tag=x_table_tags[g], align_bytes=64) for g in range(PASSES)]
+        e_table = held.tile([P, W], I32, name="e_table", align_bytes=64)
 
         def load_w(g):
             nc.sync.dma_start(out=w_raw[g][:], in_=w1[g * K_PASS : (g + 1) * K_PASS, :].rearrange("(p j) c -> p j c", j=PACK))
@@ -60,7 +64,7 @@ def tile_picked_ymatch_sum_p_kernel(tc, x_words, x_scales, w1, e_words, e_scales
         for g in range(PASSES):
             nc.sync.dma_start(
                 out=x_scale_table[64 * g : 64 * (g + 1) : 4, :].bitcast(I32),
-                in_=x_scales[g].rearrange("(q r) c -> r q c", r=4).bitcast(I32),
+                in_=x_scales[g].rearrange("(q r) c -> r q c", r=QUAD_ROWS).bitcast(I32),
             )
         nc.sync.dma_start(sup_sb[:], sup)
         nc.sync.dma_start(out=e_scale_table[0:P:8, :].bitcast(I32), in_=e_scales[0].bitcast(I32))
@@ -71,85 +75,84 @@ def tile_picked_ymatch_sum_p_kernel(tc, x_words, x_scales, w1, e_words, e_scales
         w_scale = [held.tile([P, H], U8, name=f"w_scale{g}", align_bytes=64) for g in range(PASSES)]
         w_bf = [held.tile([P, PACK, P, PACK], BF16, name=f"w_bf{g}", align_bytes=64) for g in range(PASSES)]
 
-        def round_w(g, m_scalar):
-            dst = w_bf[g][:].rearrange("p t m j -> p m t j")
-            src = w_raw[g][:].rearrange("p j (m t) -> p m t j", t=PACK)
-            nc.scalar.copy(out=dst[:, :m_scalar], in_=src[:, :m_scalar])
-            if m_scalar < P:
-                nc.vector.tensor_copy(out=dst[:, m_scalar:], in_=src[:, m_scalar:])
+        def w_views(g):
+            return w_bf[g][:].rearrange("p t m j -> p m t j"), w_raw[g][:].rearrange("p j (m t) -> p m t j", t=PACK)
 
         def quantise_w(g, tag):
             w_codes.append(held.tile([P, H], U32, name=f"w_codes{g}", tag=tag, align_bytes=64))
             nc.vector.quantize_mx(out=w_codes[g][:].bitcast(FP8X4), scales=w_scale[g][:], in_=w_bf[g][:].rearrange("p t m j -> p (t m j)"))
 
         x_scale_picked = held.tile([P, S], U8, name="x_scale_picked", align_bytes=64)
-        e_scale_picked = held.tile([P, U], U8, name="e_scale_picked", align_bytes=64)
+        e_scale_picked = held.tile([P, U], U8, name="e_scale_picked", tag="e_scale_picked_then_h_scale", align_bytes=64)
         x_codes = [[held.tile([P, HALF], U32, name=f"x_codes{g}_{u}", align_bytes=64) for u in range(2)] for g in range(PASSES)]
         e_codes = held.tile([P, U], U32, name="e_codes", align_bytes=64)
-
 
         h_ps = [psum.tile([P, PACK, Q_TILE], F32, name=f"h_ps{b}") for b in range(Q_TILES)]
         y_ps = [psum.tile([P, U], F32, name=f"y_ps{b}") for b in range(Q_TILES)]
         h_bf = held.tile([P, Q_TILES, Q_TILE, PACK], BF16, name="h_bf", align_bytes=64)
-        h_scale = held.tile([P, S], U8, name="h_scale", align_bytes=64)
+        h_codes = held.tile([P, S], U32, name="h_codes", align_bytes=64)
 
-        def gather_x(g, u):
-            cols = slice(u * HALF // 16, (u + 1) * HALF // 16)
-            nc.vector.tensor_copy(x_codes[g][u][:], x_table[g][:].bitcast(U32).indirect(offs_sb[:, cols]))
+        def gather_x(g):
+            for u in range(2):
+                cols = slice(u * HALF // LIST_ROWS, (u + 1) * HALF // LIST_ROWS)
+                nc.vector.tensor_copy(x_codes[g][u][:], x_table[g][:].bitcast(U32).indirect(offs_sb[:, cols]))
 
-        def project(g, b):
-            u, c = divmod(b * Q_TILE, HALF)
-            for t in range(PACK):
-                nc.tensor.matmul_mx(
-                    out=h_ps[b][:, t, :],
-                    lhsT=w_codes[g][:, t * P : (t + 1) * P].bitcast(FP8X4),
-                    lhsT_scale=w_scale[g][:, t * P : (t + 1) * P],
-                    rhs=x_codes[g][u][:, c : c + Q_TILE].bitcast(FP8X4),
-                    rhs_scale=x_scale[4 * g : P, b * Q_TILE : (b + 1) * Q_TILE],
-                    start=(g == 0 and t == 0),
-                    stop=(g == PASSES - 1 and t == PACK - 1),
-                )
+        def project(g):
+            for b in range(Q_TILES):
+                u, c = divmod(b * Q_TILE, HALF)
+                for t in range(PACK):
+                    nc.tensor.matmul_mx(
+                        out=h_ps[b][:, t, :],
+                        lhsT=w_codes[g][:, t * P : (t + 1) * P].bitcast(FP8X4),
+                        lhsT_scale=w_scale[g][:, t * P : (t + 1) * P],
+                        rhs=x_codes[g][u][:, c : c + Q_TILE].bitcast(FP8X4),
+                        rhs_scale=x_scale[QUAD_ROWS * g : P, b * Q_TILE : (b + 1) * Q_TILE],
+                        start=(g == 0 and t == 0),
+                        stop=(g == PASSES - 1 and t == PACK - 1),
+                    )
 
-        round_w(0, M_SCALAR)
+        rounded, raw = w_views(0)
+        nc.scalar.copy(out=rounded[:, :SCALAR_GROUPS_PASS0], in_=raw[:, :SCALAR_GROUPS_PASS0])
+        nc.vector.tensor_copy(out=rounded[:, SCALAR_GROUPS_PASS0:], in_=raw[:, SCALAR_GROUPS_PASS0:])
+
         nc.vector.tensor_copy(x_scale_picked[:], x_scale_table[:].indirect(offs_sb[:]))
         for q in range(QUADS):
-            nc.sync.dma_start(out=x_scale[32 * q : 32 * q + 8, :].bitcast(I32), in_=x_scale_picked[4 * q : P : 16, :].bitcast(I32))
+            nc.sync.dma_start(
+                out=x_scale[32 * q : 32 * q + PASSES * QUAD_ROWS, :].bitcast(I32), in_=x_scale_picked[4 * q : P : 16, :].bitcast(I32)
+            )
         load_words(x_table[1], x_words[1])
         load_words(e_table, e_words[0])
         nc.vector.tensor_copy(e_scale_picked[:], e_scale_table[:].indirect(sup_sb[:]))
-        for r in range(4):
+        for r in range(QUAD_ROWS):
             nc.sync.dma_start(out=e_scale[r:P:32, :].bitcast(I32), in_=e_scale_picked[8 * r : P : 32, :].bitcast(I32))
-        quantise_w(0, "e_scale_table")
-        round_w(1, P)
-        for u in range(2):
-            gather_x(0, u)
-        for b in range(Q_TILES):
-            project(0, b)
-        quantise_w(1, "x_table0")
-        for u in range(2):
-            gather_x(1, u)
-        for b in range(Q_TILES):
-            project(1, b)
 
-        def quantise_h(codes, scales, lo, hi):
-            nc.vector.quantize_mx(out=codes.bitcast(FP8X4), scales=scales, in_=h_bf[:, lo:hi].rearrange("p b q t -> p (b q t)"))
+        quantise_w(0, "e_scale_table_then_w_codes0")
+        rounded, raw = w_views(1)
+        nc.scalar.copy(out=rounded, in_=raw)
+        gather_x(0)
+        project(0)
+        quantise_w(1, "x_table0_then_w_codes1")
+        gather_x(1)
+        project(1)
 
-        for b in range(Q_TILES):
+        nc.vector.tensor_copy(out=h_bf[:, 0], in_=h_ps[0][:].rearrange("p t q -> p q t"))
+        for b in range(1, Q_TILES):
             nc.scalar.copy(out=h_bf[:, b], in_=h_ps[b][:].rearrange("p t q -> p q t"))
 
-        h_codes_first = held.tile([P, Q_TILE], U32, name="h_codes_first", align_bytes=64)
-        quantise_h(h_codes_first[:], h_scale[:, :Q_TILE], 0, 1)
         nc.vector.tensor_copy(e_codes[:], e_table[:].bitcast(U32).indirect(sup_sb[:]))
-        h_codes_rest = held.tile([P, S - Q_TILE], U32, name="h_codes_rest", tag="e_table_then_h_codes", align_bytes=64)
-        quantise_h(h_codes_rest[:, :Q_TILE], h_scale[:, Q_TILE:HALF], 1, 2)
-        quantise_h(h_codes_rest[:, Q_TILE:], h_scale[:, HALF:], 2, 4)
-        h_codes = [h_codes_first[:]] + [h_codes_rest[:, (b - 1) * Q_TILE : b * Q_TILE] for b in range(1, Q_TILES)]
+        h_scale = held.tile([P, S], U8, name="h_scale", tag="e_scale_picked_then_h_scale", align_bytes=64)
+        for lo, hi in ((0, 1), (1, 2), (2, Q_TILES)):
+            cols = slice(lo * Q_TILE, hi * Q_TILE)
+            nc.vector.quantize_mx(
+                out=h_codes[:, cols].bitcast(FP8X4), scales=h_scale[:, cols], in_=h_bf[:, lo:hi].rearrange("p b q t -> p (b q t)")
+            )
 
         for b in range(Q_TILES):
+            cols = slice(b * Q_TILE, (b + 1) * Q_TILE)
             nc.tensor.matmul_mx(
                 out=y_ps[b][:],
-                lhsT=h_codes[b].bitcast(FP8X4),
-                lhsT_scale=h_scale[:, b * Q_TILE : (b + 1) * Q_TILE],
+                lhsT=h_codes[:, cols].bitcast(FP8X4),
+                lhsT_scale=h_scale[:, cols],
                 rhs=e_codes[:].bitcast(FP8X4),
                 rhs_scale=e_scale[:],
                 start=True,
@@ -160,11 +163,13 @@ def tile_picked_ymatch_sum_p_kernel(tc, x_words, x_scales, w1, e_words, e_scales
             neg_max = held.tile([P, 1], F32, name=f"neg_max{b}")
             total = held.tile([P, 1], F32, name=f"total{b}")
             inv = held.tile([P, 1], F32, name=f"inv{b}")
-            ex = held.tile([P, D, U // D], F32, name=f"ex{b}")
-            pair = held.tile([P, U // D], F32, name=f"pair{b}")
-            prob = held.tile([P, U // D], F32, name=f"prob{b}")
+            ex = held.tile([P, D, CLASSES], F32, name=f"ex{b}")
+            pair = held.tile([P, CLASSES], F32, name=f"pair{b}")
+            prob = held.tile([P, CLASSES], F32, name=f"prob{b}")
             nc.vector.tensor_reduce(out=neg_max[:], in_=y_ps[b][:], axis=mybir.AxisListType.X, op=ALU.max, negate=True)
-            nc.scalar.activation(out=ex[:], in_=y_ps[b][:].rearrange("p (v d) -> p d v", d=D), func=ACT.Exp, bias=neg_max[:], scale=1.0, accum_out=total[:])
+            nc.scalar.activation(
+                out=ex[:], in_=y_ps[b][:].rearrange("p (v d) -> p d v", d=D), func=ACT.Exp, bias=neg_max[:], scale=1.0, accum_out=total[:]
+            )
             nc.vector.reciprocal(out=inv[:], in_=total[:])
             nc.vector.tensor_tensor(out=pair[:], in0=ex[:, 0, :], in1=ex[:, 1, :], op=ALU.add)
             if b < Q_TILES - 1:

@@ -41,7 +41,8 @@ def tile_picked_ymatch_sum_p_kernel(tc, x_words, x_scales, w1, e_words, e_scales
 
         x_scale_table = held.tile([P, T], U8, name="x_scale_table", align_bytes=64)
         e_scale_table = held.tile([P, W], U8, name="e_scale_table", tag="e_scale_table_then_w_codes0", align_bytes=64)
-        nc.gpsimd.memset(x_scale_table[:].bitcast(I32), 0)
+        nc.vector.memset(x_scale_table[32:64, :].bitcast(I32), 0)
+        nc.vector.memset(x_scale_table[64:P, :].bitcast(I32), 0)
         nc.vector.memset(e_scale_table[:].bitcast(I32), 0)
         x_scale = held.tile([P, S], U8, name="x_scale", align_bytes=64)
         e_scale = held.tile([P, U], U8, name="e_scale", align_bytes=64)
@@ -59,13 +60,13 @@ def tile_picked_ymatch_sum_p_kernel(tc, x_words, x_scales, w1, e_words, e_scales
         def load_words(table, words):
             nc.sync.dma_start(out=table[:], in_=words.rearrange("p n j -> p (n j)").bitcast(I32))
 
-        load_w(0)
-        nc.sync.dma_start(offs_sb[:], offs)
         for g in range(PASSES):
             nc.sync.dma_start(
-                out=x_scale_table[64 * g : 64 * (g + 1) : 4, :].bitcast(I32),
+                out=x_scale_table[16 * g : 16 * (g + 1), :].bitcast(I32),
                 in_=x_scales[g].rearrange("(q r) c -> r q c", r=QUAD_ROWS).bitcast(I32),
             )
+        nc.sync.dma_start(offs_sb[:], offs)
+        load_w(0)
         nc.sync.dma_start(sup_sb[:], sup)
         nc.sync.dma_start(out=e_scale_table[0:P:8, :].bitcast(I32), in_=e_scales[0].bitcast(I32))
         load_w(1)
@@ -118,7 +119,7 @@ def tile_picked_ymatch_sum_p_kernel(tc, x_words, x_scales, w1, e_words, e_scales
         nc.vector.tensor_copy(x_scale_picked[:], x_scale_table[:].indirect(offs_sb[:]))
         for q in range(QUADS):
             nc.sync.dma_start(
-                out=x_scale[32 * q : 32 * q + PASSES * QUAD_ROWS, :].bitcast(I32), in_=x_scale_picked[4 * q : P : 16, :].bitcast(I32)
+                out=x_scale[32 * q : 32 * q + PASSES * QUAD_ROWS, :].bitcast(I32), in_=x_scale_picked[q:32:4, :].bitcast(I32)
             )
         load_words(x_table[1], x_words[1])
         load_words(e_table, e_words[0])
@@ -159,21 +160,55 @@ def tile_picked_ymatch_sum_p_kernel(tc, x_words, x_scales, w1, e_words, e_scales
                 stop=True,
             )
 
-        for b in range(Q_TILES):
-            neg_max = held.tile([P, 1], F32, name=f"neg_max{b}")
-            total = held.tile([P, 1], F32, name=f"total{b}")
-            inv = held.tile([P, 1], F32, name=f"inv{b}")
-            ex = held.tile([P, D, CLASSES], F32, name=f"ex{b}")
-            pair = held.tile([P, CLASSES], F32, name=f"pair{b}")
-            prob = held.tile([P, CLASSES], F32, name=f"prob{b}")
-            nc.vector.tensor_reduce(out=neg_max[:], in_=y_ps[b][:], axis=mybir.AxisListType.X, op=ALU.max, negate=True)
+        neg_max = [held.tile([P, 1], F32, name=f"neg_max{b}") for b in range(Q_TILES)]
+        total = held.tile([P, Q_TILES], F32, name="total")
+        inv = held.tile([P, Q_TILES], F32, name="inv")
+        ex = [held.tile([P, D, CLASSES], F32, name=f"ex{b}") for b in range(Q_TILES)]
+        pair = [held.tile([P, CLASSES], F32, name=f"pair{b}") for b in range(Q_TILES)]
+        prob = [held.tile([P, CLASSES], F32, name=f"prob{b}") for b in range(Q_TILES)]
+
+        def row_max(b):
+            nc.vector.tensor_reduce(out=neg_max[b][:], in_=y_ps[b][:], axis=mybir.AxisListType.X, op=ALU.max, negate=True)
             nc.scalar.activation(
-                out=ex[:], in_=y_ps[b][:].rearrange("p (v d) -> p d v", d=D), func=ACT.Exp, bias=neg_max[:], scale=1.0, accum_out=total[:]
+                out=ex[b][:],
+                in_=y_ps[b][:].rearrange("p (v d) -> p d v", d=D),
+                func=ACT.Exp,
+                bias=neg_max[b][:],
+                scale=1.0,
+                accum_out=total[:, b : b + 1],
             )
-            nc.vector.reciprocal(out=inv[:], in_=total[:])
-            nc.vector.tensor_tensor(out=pair[:], in0=ex[:, 0, :], in1=ex[:, 1, :], op=ALU.add)
-            if b < Q_TILES - 1:
-                nc.scalar.activation(out=prob[:], in_=pair[:], func=ACT.Copy, scale=inv[:])
-            else:
-                nc.vector.tensor_scalar(out=prob[:], in0=pair[:], scalar1=inv[:], scalar2=None, op0=ALU.mult)
-            nc.sync.dma_start(out=out[b * Q_TILE : (b + 1) * Q_TILE, :], in_=prob[:])
+
+        def invert(lo, hi):
+            nc.vector.reciprocal(out=inv[:, lo:hi], in_=total[:, lo:hi])
+
+        def add_pairs(engine, b):
+            engine.tensor_tensor(out=pair[b][:], in0=ex[b][:, 0, :], in1=ex[b][:, 1, :], op=ALU.add)
+
+        def scale_rows(engine, b):
+            engine.tensor_scalar(out=prob[b][:], in0=pair[b][:], scalar1=inv[:, b : b + 1], scalar2=None, op0=ALU.mult)
+
+        def store(b):
+            nc.sync.dma_start(out=out[b * Q_TILE : (b + 1) * Q_TILE, :], in_=prob[b][:])
+
+        def scale_rows_on_scalar(b):
+            nc.scalar.activation(out=prob[b][:], in_=pair[b][:], func=ACT.Copy, scale=inv[:, b : b + 1])
+
+        for b in range(Q_TILES):
+            row_max(b)
+        add_pairs(nc.gpsimd, 0)
+        invert(0, 2)
+        add_pairs(nc.vector, 1)
+        scale_rows(nc.vector, 0)
+        store(0)
+        invert(2, 3)
+        add_pairs(nc.vector, 2)
+        for b in (1, 2):
+            scale_rows_on_scalar(b)
+            store(b)
+        invert(3, 4)
+        halves = [slice(u * CLASSES // 2, (u + 1) * CLASSES // 2) for u in range(2)]
+        for cols in halves:
+            nc.vector.tensor_tensor(out=pair[3][:, cols], in0=ex[3][:, 0, cols], in1=ex[3][:, 1, cols], op=ALU.add)
+        for cols in halves:
+            nc.vector.tensor_scalar(out=prob[3][:, cols], in0=pair[3][:, cols], scalar1=inv[:, 3:4], scalar2=None, op0=ALU.mult)
+            nc.sync.dma_start(out=out[3 * Q_TILE :, cols], in_=prob[3][:, cols])

@@ -86,7 +86,7 @@ def tile_picked_ymatch_sum_p_kernel(tc, x_words, x_scales, w1, e_words, e_scales
         x_scale_picked = held.tile([P, S], U8, name="x_scale_picked", align_bytes=64)
         e_scale_picked = held.tile([P, U], U8, name="e_scale_picked", tag="e_scale_picked_then_h_scale", align_bytes=64)
         x_codes = [[held.tile([P, HALF], U32, name=f"x_codes{g}_{u}", align_bytes=64) for u in range(2)] for g in range(PASSES)]
-        e_codes = held.tile([P, U], U32, name="e_codes", align_bytes=64)
+        e_codes = [held.tile([P, U // 2], U32, name=f"e_codes{u}", align_bytes=64) for u in range(2)]
 
         h_ps = [psum.tile([P, PACK, Q_TILE], F32, name=f"h_ps{b}") for b in range(Q_TILES)]
         y_ps = [psum.tile([P, U], F32, name=f"y_ps{b}") for b in range(Q_TILES)]
@@ -136,29 +136,37 @@ def tile_picked_ymatch_sum_p_kernel(tc, x_words, x_scales, w1, e_words, e_scales
         gather_x(1)
         project(1)
 
-        nc.vector.tensor_copy(out=h_bf[:, 0], in_=h_ps[0][:].rearrange("p t q -> p q t"))
-        for b in range(1, Q_TILES):
+        for b in range(Q_TILES):
             nc.scalar.copy(out=h_bf[:, b], in_=h_ps[b][:].rearrange("p t q -> p q t"))
 
-        nc.vector.tensor_copy(e_codes[:], e_table[:].bitcast(U32).indirect(sup_sb[:]))
-        h_scale = held.tile([P, S], U8, name="h_scale", tag="e_scale_picked_then_h_scale", align_bytes=64)
-        for lo, hi in ((0, 1), (1, 2), (2, Q_TILES)):
+        def quantise_h(scale, lo, hi):
             cols = slice(lo * Q_TILE, hi * Q_TILE)
             nc.vector.quantize_mx(
-                out=h_codes[:, cols].bitcast(FP8X4), scales=h_scale[:, cols], in_=h_bf[:, lo:hi].rearrange("p b q t -> p (b q t)")
+                out=h_codes[:, cols].bitcast(FP8X4), scales=scale[:, cols], in_=h_bf[:, lo:hi].rearrange("p b q t -> p (b q t)")
             )
+
+        h_scale_first = held.tile([P, Q_TILE], U8, name="h_scale_first", align_bytes=64)
+        quantise_h(h_scale_first, 0, 1)
+        for u in range(2):
+            cols = slice(u * U // 2 // LIST_ROWS, (u + 1) * U // 2 // LIST_ROWS)
+            nc.vector.tensor_copy(e_codes[u][:], e_table[:].bitcast(U32).indirect(sup_sb[:, cols]))
+        h_scale = held.tile([P, S], U8, name="h_scale", tag="e_scale_picked_then_h_scale", align_bytes=64)
+        quantise_h(h_scale, 1, 2)
+        quantise_h(h_scale, 2, Q_TILES)
 
         for b in range(Q_TILES):
             cols = slice(b * Q_TILE, (b + 1) * Q_TILE)
-            nc.tensor.matmul_mx(
-                out=y_ps[b][:],
-                lhsT=h_codes[:, cols].bitcast(FP8X4),
-                lhsT_scale=h_scale[:, cols],
-                rhs=e_codes[:].bitcast(FP8X4),
-                rhs_scale=e_scale[:],
-                start=True,
-                stop=True,
-            )
+            for u in range(2):
+                half = slice(u * U // 2, (u + 1) * U // 2)
+                nc.tensor.matmul_mx(
+                    out=y_ps[b][:, half],
+                    lhsT=h_codes[:, cols].bitcast(FP8X4),
+                    lhsT_scale=(h_scale_first if b == 0 else h_scale)[:, cols],
+                    rhs=e_codes[u][:].bitcast(FP8X4),
+                    rhs_scale=e_scale[:, half],
+                    start=True,
+                    stop=True,
+                )
 
         neg_max = [held.tile([P, 1], F32, name=f"neg_max{b}") for b in range(Q_TILES)]
         total = held.tile([P, Q_TILES], F32, name="total")

@@ -26,7 +26,7 @@ Q_TILE = 128
 Q_TILES = S // Q_TILE
 HALF = S // 2
 CLASSES = U // D
-SCALAR_GROUPS_PASS0 = 88
+SCALAR_GROUPS = (64, 44)
 
 
 def tile_picked_ymatch_sum_p_kernel(tc, x_words, x_scales, w1, e_words, e_scales, offs, sup, out):
@@ -34,25 +34,35 @@ def tile_picked_ymatch_sum_p_kernel(tc, x_words, x_scales, w1, e_words, e_scales
     with ExitStack() as ctx:
         lists = ctx.enter_context(tc.tile_pool(name="lists", bufs=1))
         held = ctx.enter_context(tc.tile_pool(name="held", bufs=1))
+        reused = ctx.enter_context(tc.tile_pool(name="reused", bufs=1))
         psum = ctx.enter_context(tc.psum_pool(name="psum", bufs=1))
 
         offs_sb = lists.tile([P, S // LIST_ROWS], U16, name="offs_sb")
         sup_sb = lists.tile([P, U // LIST_ROWS], U16, name="sup_sb")
 
         x_scale_table = held.tile([P, T], U8, name="x_scale_table", align_bytes=64)
-        e_scale_table = held.tile([P, W], U8, name="e_scale_table", tag="e_scale_table_then_w_codes0", align_bytes=64)
-        nc.vector.memset(x_scale_table[32:64, :].bitcast(I32), 0)
-        nc.vector.memset(x_scale_table[64:P, :].bitcast(I32), 0)
-        nc.vector.memset(e_scale_table[:].bitcast(I32), 0)
+        e_scale_table = held.tile([P, W], U8, name="e_scale_table", align_bytes=64)
         x_scale = held.tile([P, S], U8, name="x_scale", align_bytes=64)
         e_scale = held.tile([P, U], U8, name="e_scale", align_bytes=64)
+        nc.vector.memset(e_scale_table[:].bitcast(I32), 0)
+        nc.vector.memset(x_scale_table[32:64, :].bitcast(I32), 0)
+        nc.vector.memset(x_scale_table[64:P, :].bitcast(I32), 0)
         nc.vector.memset(x_scale[:].bitcast(I32), 0)
         nc.vector.memset(e_scale[:].bitcast(I32), 0)
 
         w_raw = [held.tile([P, PACK, H], F32, name=f"w_raw{g}") for g in range(PASSES)]
-        x_table_tags = ("x_table0_then_w_codes1", "x_table1")
-        x_table = [held.tile([P, T], I32, name=f"x_table{g}", tag=x_table_tags[g], align_bytes=64) for g in range(PASSES)]
+        x_table = [held.tile([P, T], I32, name=f"x_table{g}", align_bytes=64) for g in range(PASSES)]
         e_table = held.tile([P, W], I32, name="e_table", align_bytes=64)
+        w_bf = [held.tile([P, PACK, P, PACK], BF16, name=f"w_bf{g}", align_bytes=64) for g in range(PASSES)]
+        w_codes = [held.tile([P, H], U32, name=f"w_codes{g}", align_bytes=64) for g in range(PASSES)]
+        w_scale = [held.tile([P, H], U8, name=f"w_scale{g}", align_bytes=64) for g in range(PASSES)]
+        x_scale_picked = held.tile([P, S], U8, name="x_scale_picked", align_bytes=64)
+        e_scale_picked = reused.tile([P, U], U8, name="e_scale_picked", offset=U // 2, align_bytes=64)
+        x_codes = [[held.tile([P, HALF], U32, name=f"x_codes{g}_{u}", align_bytes=64) for u in range(2)] for g in range(PASSES)]
+        h_ps = [psum.tile([P, PACK, Q_TILE], F32, name=f"h_ps{b}") for b in range(Q_TILES)]
+        y_ps = [psum.tile([P, U], F32, name=f"y_ps{b}") for b in range(Q_TILES)]
+        h_bf = held.tile([P, Q_TILES, Q_TILE, PACK], BF16, name="h_bf", align_bytes=64)
+        h_codes = held.tile([P, S], U32, name="h_codes", align_bytes=64)
 
         def load_w(g):
             nc.sync.dma_start(out=w_raw[g][:], in_=w1[g * K_PASS : (g + 1) * K_PASS, :].rearrange("(p j) c -> p j c", j=PACK))
@@ -60,38 +70,14 @@ def tile_picked_ymatch_sum_p_kernel(tc, x_words, x_scales, w1, e_words, e_scales
         def load_words(table, words):
             nc.sync.dma_start(out=table[:], in_=words.rearrange("p n j -> p (n j)").bitcast(I32))
 
-        for g in range(PASSES):
-            nc.sync.dma_start(
-                out=x_scale_table[16 * g : 16 * (g + 1), :].bitcast(I32),
-                in_=x_scales[g].rearrange("(q r) c -> r q c", r=QUAD_ROWS).bitcast(I32),
-            )
-        nc.sync.dma_start(offs_sb[:], offs)
-        load_w(0)
-        nc.sync.dma_start(sup_sb[:], sup)
-        nc.sync.dma_start(out=e_scale_table[0:P:8, :].bitcast(I32), in_=e_scales[0].bitcast(I32))
-        load_w(1)
-        load_words(x_table[0], x_words[0])
+        def round_w(g):
+            rounded = w_bf[g][:].rearrange("p t m j -> p m t j")
+            raw = w_raw[g][:].rearrange("p j (m t) -> p m t j", t=PACK)
+            nc.scalar.copy(out=rounded[:, :SCALAR_GROUPS[g]], in_=raw[:, :SCALAR_GROUPS[g]])
+            nc.vector.tensor_copy(out=rounded[:, SCALAR_GROUPS[g] :], in_=raw[:, SCALAR_GROUPS[g] :])
 
-        w_codes = []
-        w_scale = [held.tile([P, H], U8, name=f"w_scale{g}", align_bytes=64) for g in range(PASSES)]
-        w_bf = [held.tile([P, PACK, P, PACK], BF16, name=f"w_bf{g}", align_bytes=64) for g in range(PASSES)]
-
-        def w_views(g):
-            return w_bf[g][:].rearrange("p t m j -> p m t j"), w_raw[g][:].rearrange("p j (m t) -> p m t j", t=PACK)
-
-        def quantise_w(g, tag):
-            w_codes.append(held.tile([P, H], U32, name=f"w_codes{g}", tag=tag, align_bytes=64))
+        def quantise_w(g):
             nc.vector.quantize_mx(out=w_codes[g][:].bitcast(FP8X4), scales=w_scale[g][:], in_=w_bf[g][:].rearrange("p t m j -> p (t m j)"))
-
-        x_scale_picked = held.tile([P, S], U8, name="x_scale_picked", align_bytes=64)
-        e_scale_picked = held.tile([P, U], U8, name="e_scale_picked", tag="e_scale_picked_then_h_scale", align_bytes=64)
-        x_codes = [[held.tile([P, HALF], U32, name=f"x_codes{g}_{u}", align_bytes=64) for u in range(2)] for g in range(PASSES)]
-        e_codes = [held.tile([P, U // 2], U32, name=f"e_codes{u}", align_bytes=64) for u in range(2)]
-
-        h_ps = [psum.tile([P, PACK, Q_TILE], F32, name=f"h_ps{b}") for b in range(Q_TILES)]
-        y_ps = [psum.tile([P, U], F32, name=f"y_ps{b}") for b in range(Q_TILES)]
-        h_bf = held.tile([P, Q_TILES, Q_TILE, PACK], BF16, name="h_bf", align_bytes=64)
-        h_codes = held.tile([P, S], U32, name="h_codes", align_bytes=64)
 
         def gather_x(g):
             for u in range(2):
@@ -112,47 +98,61 @@ def tile_picked_ymatch_sum_p_kernel(tc, x_words, x_scales, w1, e_words, e_scales
                         stop=(g == PASSES - 1 and t == PACK - 1),
                     )
 
-        rounded, raw = w_views(0)
-        nc.scalar.copy(out=rounded[:, :SCALAR_GROUPS_PASS0], in_=raw[:, :SCALAR_GROUPS_PASS0])
-        nc.vector.tensor_copy(out=rounded[:, SCALAR_GROUPS_PASS0:], in_=raw[:, SCALAR_GROUPS_PASS0:])
+        for g in range(PASSES):
+            nc.sync.dma_start(
+                out=x_scale_table[16 * g : 16 * (g + 1), :].bitcast(I32),
+                in_=x_scales[g].rearrange("(q r) c -> r q c", r=QUAD_ROWS).bitcast(I32),
+            )
+        nc.sync.dma_start(offs_sb[:], offs)
+        load_words(x_table[0], x_words[0])
+        nc.sync.dma_start(sup_sb[:], sup)
+        nc.sync.dma_start(out=e_scale_table[0:P:8, :].bitcast(I32), in_=e_scales[0].bitcast(I32))
+        load_w(0)
 
         nc.vector.tensor_copy(x_scale_picked[:], x_scale_table[:].indirect(offs_sb[:]))
         for q in range(QUADS):
             nc.sync.dma_start(
                 out=x_scale[32 * q : 32 * q + PASSES * QUAD_ROWS, :].bitcast(I32), in_=x_scale_picked[q:32:4, :].bitcast(I32)
             )
+        load_w(1)
         load_words(x_table[1], x_words[1])
         load_words(e_table, e_words[0])
+        gather_x(0)
         nc.vector.tensor_copy(e_scale_picked[:], e_scale_table[:].indirect(sup_sb[:]))
         for r in range(QUAD_ROWS):
             nc.sync.dma_start(out=e_scale[r:P:32, :].bitcast(I32), in_=e_scale_picked[8 * r : P : 32, :].bitcast(I32))
 
-        quantise_w(0, "e_scale_table_then_w_codes0")
-        rounded, raw = w_views(1)
-        nc.scalar.copy(out=rounded, in_=raw)
-        gather_x(0)
+        round_w(0)
+        quantise_w(0)
         project(0)
-        quantise_w(1, "x_table0_then_w_codes1")
+        round_w(1)
+        quantise_w(1)
         gather_x(1)
         project(1)
 
         for b in range(Q_TILES):
             nc.scalar.copy(out=h_bf[:, b], in_=h_ps[b][:].rearrange("p t q -> p q t"))
 
-        def quantise_h(scale, lo, hi):
+        def quantise_h(lo, hi):
             cols = slice(lo * Q_TILE, hi * Q_TILE)
             nc.vector.quantize_mx(
-                out=h_codes[:, cols].bitcast(FP8X4), scales=scale[:, cols], in_=h_bf[:, lo:hi].rearrange("p b q t -> p (b q t)")
+                out=h_codes[:, cols].bitcast(FP8X4), scales=h_scale[:, cols], in_=h_bf[:, lo:hi].rearrange("p b q t -> p (b q t)")
             )
 
-        h_scale_first = held.tile([P, Q_TILE], U8, name="h_scale_first", align_bytes=64)
-        quantise_h(h_scale_first, 0, 1)
-        for u in range(2):
+        def gather_e(u):
             cols = slice(u * U // 2 // LIST_ROWS, (u + 1) * U // 2 // LIST_ROWS)
             nc.vector.tensor_copy(e_codes[u][:], e_table[:].bitcast(U32).indirect(sup_sb[:, cols]))
-        h_scale = held.tile([P, S], U8, name="h_scale", tag="e_scale_picked_then_h_scale", align_bytes=64)
-        quantise_h(h_scale, 1, 2)
-        quantise_h(h_scale, 2, Q_TILES)
+
+        h_scale = reused.tile([P, S], U8, name="h_scale", offset=0, align_bytes=64)
+        e_codes = [
+            held.tile([P, U // 2], U32, name="e_codes0", align_bytes=64),
+            reused.tile([P, U // 2], U32, name="e_codes1", offset=S, align_bytes=64),
+        ]
+        gather_e(0)
+        quantise_h(0, 1)
+        gather_e(1)
+        quantise_h(1, 2)
+        quantise_h(2, Q_TILES)
 
         for b in range(Q_TILES):
             cols = slice(b * Q_TILE, (b + 1) * Q_TILE)
@@ -161,7 +161,7 @@ def tile_picked_ymatch_sum_p_kernel(tc, x_words, x_scales, w1, e_words, e_scales
                 nc.tensor.matmul_mx(
                     out=y_ps[b][:, half],
                     lhsT=h_codes[:, cols].bitcast(FP8X4),
-                    lhsT_scale=(h_scale_first if b == 0 else h_scale)[:, cols],
+                    lhsT_scale=h_scale[:, cols],
                     rhs=e_codes[u][:].bitcast(FP8X4),
                     rhs_scale=e_scale[:, half],
                     start=True,

@@ -24,9 +24,9 @@ QUAD_ROWS = 4
 LIST_ROWS = 16
 Q_TILE = 128
 Q_TILES = S // Q_TILE
-HALF = S // 2
+GATHER_TILES = ((4,), (1, 1, 2))
 CLASSES = U // D
-SCALAR_GROUPS = (64, 44)
+SCALAR_GROUPS = 44
 
 
 def tile_picked_ymatch_sum_p_kernel(tc, x_words, x_scales, w1, e_words, e_scales, offs, sup, out):
@@ -34,7 +34,6 @@ def tile_picked_ymatch_sum_p_kernel(tc, x_words, x_scales, w1, e_words, e_scales
     with ExitStack() as ctx:
         lists = ctx.enter_context(tc.tile_pool(name="lists", bufs=1))
         held = ctx.enter_context(tc.tile_pool(name="held", bufs=1))
-        reused = ctx.enter_context(tc.tile_pool(name="reused", bufs=1))
         psum = ctx.enter_context(tc.psum_pool(name="psum", bufs=1))
 
         offs_sb = lists.tile([P, S // LIST_ROWS], U16, name="offs_sb")
@@ -57,8 +56,9 @@ def tile_picked_ymatch_sum_p_kernel(tc, x_words, x_scales, w1, e_words, e_scales
         w_codes = [held.tile([P, H], U32, name=f"w_codes{g}", align_bytes=64) for g in range(PASSES)]
         w_scale = [held.tile([P, H], U8, name=f"w_scale{g}", align_bytes=64) for g in range(PASSES)]
         x_scale_picked = held.tile([P, S], U8, name="x_scale_picked", align_bytes=64)
-        e_scale_picked = reused.tile([P, U], U8, name="e_scale_picked", offset=U // 2, align_bytes=64)
-        x_codes = [[held.tile([P, HALF], U32, name=f"x_codes{g}_{u}", align_bytes=64) for u in range(2)] for g in range(PASSES)]
+        e_scale_picked = held.tile([P, U], U8, name="e_scale_picked", tag="e_scale_picked_then_h_scale", align_bytes=64)
+        x_codes = [held.tile([P, S], U32, name=f"x_codes{g}", align_bytes=64) for g in range(PASSES)]
+        e_codes = [held.tile([P, U // 2], U32, name=f"e_codes{u}", align_bytes=64) for u in range(2)]
         h_ps = [psum.tile([P, PACK, Q_TILE], F32, name=f"h_ps{b}") for b in range(Q_TILES)]
         y_ps = [psum.tile([P, U], F32, name=f"y_ps{b}") for b in range(Q_TILES)]
         h_bf = held.tile([P, Q_TILES, Q_TILE, PACK], BF16, name="h_bf", align_bytes=64)
@@ -73,26 +73,28 @@ def tile_picked_ymatch_sum_p_kernel(tc, x_words, x_scales, w1, e_words, e_scales
         def round_w(g):
             rounded = w_bf[g][:].rearrange("p t m j -> p m t j")
             raw = w_raw[g][:].rearrange("p j (m t) -> p m t j", t=PACK)
-            nc.scalar.copy(out=rounded[:, :SCALAR_GROUPS[g]], in_=raw[:, :SCALAR_GROUPS[g]])
-            nc.vector.tensor_copy(out=rounded[:, SCALAR_GROUPS[g] :], in_=raw[:, SCALAR_GROUPS[g] :])
+            nc.scalar.copy(out=rounded[:, :SCALAR_GROUPS], in_=raw[:, :SCALAR_GROUPS])
+            nc.vector.tensor_copy(out=rounded[:, SCALAR_GROUPS:], in_=raw[:, SCALAR_GROUPS:])
 
         def quantise_w(g):
             nc.vector.quantize_mx(out=w_codes[g][:].bitcast(FP8X4), scales=w_scale[g][:], in_=w_bf[g][:].rearrange("p t m j -> p (t m j)"))
 
         def gather_x(g):
-            for u in range(2):
-                cols = slice(u * HALF // LIST_ROWS, (u + 1) * HALF // LIST_ROWS)
-                nc.vector.tensor_copy(x_codes[g][u][:], x_table[g][:].bitcast(U32).indirect(offs_sb[:, cols]))
+            lo = 0
+            for tiles in GATHER_TILES[g]:
+                hi = lo + tiles * Q_TILE
+                picked = x_table[g][:].bitcast(U32).indirect(offs_sb[:, lo // LIST_ROWS : hi // LIST_ROWS])
+                nc.vector.tensor_copy(x_codes[g][:, lo:hi], picked)
+                lo = hi
 
         def project(g):
             for b in range(Q_TILES):
-                u, c = divmod(b * Q_TILE, HALF)
                 for t in range(PACK):
                     nc.tensor.matmul_mx(
                         out=h_ps[b][:, t, :],
                         lhsT=w_codes[g][:, t * P : (t + 1) * P].bitcast(FP8X4),
                         lhsT_scale=w_scale[g][:, t * P : (t + 1) * P],
-                        rhs=x_codes[g][u][:, c : c + Q_TILE].bitcast(FP8X4),
+                        rhs=x_codes[g][:, b * Q_TILE : (b + 1) * Q_TILE].bitcast(FP8X4),
                         rhs_scale=x_scale[QUAD_ROWS * g : P, b * Q_TILE : (b + 1) * Q_TILE],
                         start=(g == 0 and t == 0),
                         stop=(g == PASSES - 1 and t == PACK - 1),
@@ -133,26 +135,20 @@ def tile_picked_ymatch_sum_p_kernel(tc, x_words, x_scales, w1, e_words, e_scales
         for b in range(Q_TILES):
             nc.scalar.copy(out=h_bf[:, b], in_=h_ps[b][:].rearrange("p t q -> p q t"))
 
-        def quantise_h(lo, hi):
+        def quantise_h(scale, lo, hi):
             cols = slice(lo * Q_TILE, hi * Q_TILE)
             nc.vector.quantize_mx(
-                out=h_codes[:, cols].bitcast(FP8X4), scales=h_scale[:, cols], in_=h_bf[:, lo:hi].rearrange("p b q t -> p (b q t)")
+                out=h_codes[:, cols].bitcast(FP8X4), scales=scale[:, cols], in_=h_bf[:, lo:hi].rearrange("p b q t -> p (b q t)")
             )
 
-        def gather_e(u):
+        h_scale_first = held.tile([P, Q_TILE], U8, name="h_scale_first", align_bytes=64)
+        quantise_h(h_scale_first, 0, 1)
+        for u in range(2):
             cols = slice(u * U // 2 // LIST_ROWS, (u + 1) * U // 2 // LIST_ROWS)
             nc.vector.tensor_copy(e_codes[u][:], e_table[:].bitcast(U32).indirect(sup_sb[:, cols]))
-
-        h_scale = reused.tile([P, S], U8, name="h_scale", offset=0, align_bytes=64)
-        e_codes = [
-            held.tile([P, U // 2], U32, name="e_codes0", align_bytes=64),
-            reused.tile([P, U // 2], U32, name="e_codes1", offset=S, align_bytes=64),
-        ]
-        gather_e(0)
-        quantise_h(0, 1)
-        gather_e(1)
-        quantise_h(1, 2)
-        quantise_h(2, Q_TILES)
+        h_scale = held.tile([P, S], U8, name="h_scale", tag="e_scale_picked_then_h_scale", align_bytes=64)
+        quantise_h(h_scale, 1, 2)
+        quantise_h(h_scale, 2, Q_TILES)
 
         for b in range(Q_TILES):
             cols = slice(b * Q_TILE, (b + 1) * Q_TILE)
@@ -161,7 +157,7 @@ def tile_picked_ymatch_sum_p_kernel(tc, x_words, x_scales, w1, e_words, e_scales
                 nc.tensor.matmul_mx(
                     out=y_ps[b][:, half],
                     lhsT=h_codes[:, cols].bitcast(FP8X4),
-                    lhsT_scale=h_scale[:, cols],
+                    lhsT_scale=(h_scale_first if b == 0 else h_scale)[:, cols],
                     rhs=e_codes[u][:].bitcast(FP8X4),
                     rhs_scale=e_scale[:, half],
                     start=True,

@@ -41,7 +41,7 @@ def tile_picked_ymatch_sum_p_kernel(tc, x_words, x_scales, w1, e_words, e_scales
 
         x_scale_table = held.tile([P, T], U8, name="x_scale_table", align_bytes=64)
         e_scale_table = held.tile([P, W], U8, name="e_scale_table", align_bytes=64)
-        x_scale = held.tile([P, S], U8, name="x_scale", align_bytes=64)
+        x_scale = held.tile([P, PASSES * S], U8, name="x_scale", align_bytes=64)
         e_scale = held.tile([P, U], U8, name="e_scale", align_bytes=64)
         nc.vector.memset(e_scale_table[:].bitcast(I32), 0)
         nc.vector.memset(x_scale_table[32:64, :].bitcast(I32), 0)
@@ -95,16 +95,12 @@ def tile_picked_ymatch_sum_p_kernel(tc, x_words, x_scales, w1, e_words, e_scales
                         lhsT=w_codes[g][:, t * P : (t + 1) * P].bitcast(FP8X4),
                         lhsT_scale=w_scale[g][:, t * P : (t + 1) * P],
                         rhs=x_codes[g][:, b * Q_TILE : (b + 1) * Q_TILE].bitcast(FP8X4),
-                        rhs_scale=x_scale[QUAD_ROWS * g : P, b * Q_TILE : (b + 1) * Q_TILE],
+                        rhs_scale=x_scale[:, g * S + b * Q_TILE : g * S + (b + 1) * Q_TILE],
                         start=(g == 0 and t == 0),
                         stop=(g == PASSES - 1 and t == PACK - 1),
                     )
 
-        for g in range(PASSES):
-            nc.sync.dma_start(
-                out=x_scale_table[16 * g : 16 * (g + 1), :].bitcast(I32),
-                in_=x_scales[g].rearrange("(q r) c -> r q c", r=QUAD_ROWS).bitcast(I32),
-            )
+        nc.sync.dma_start(out=x_scale_table[0:32, :].bitcast(I32), in_=x_scales.rearrange("g j c -> j g c").bitcast(I32))
         nc.sync.dma_start(offs_sb[:], offs)
         load_words(x_table[0], x_words[0])
         nc.sync.dma_start(sup_sb[:], sup)
@@ -114,7 +110,7 @@ def tile_picked_ymatch_sum_p_kernel(tc, x_words, x_scales, w1, e_words, e_scales
         nc.vector.tensor_copy(x_scale_picked[:], x_scale_table[:].indirect(offs_sb[:]))
         for q in range(QUADS):
             nc.sync.dma_start(
-                out=x_scale[32 * q : 32 * q + PASSES * QUAD_ROWS, :].bitcast(I32), in_=x_scale_picked[q:32:4, :].bitcast(I32)
+                out=x_scale[32 * q : 32 * q + QUAD_ROWS, :].bitcast(I32), in_=x_scale_picked[8 * q : 8 * q + 8, :].bitcast(I32)
             )
         load_w(1)
         load_words(x_table[1], x_words[1])

@@ -25,6 +25,7 @@ LIST_ROWS = 16
 Q_TILE = 128
 Q_TILES = S // Q_TILE
 GATHER_TILES = ((4,), (1, 1, 2))
+LAST_SUPPORTS = 128
 CLASSES = U // D
 SCALAR_GROUPS = 44
 
@@ -58,7 +59,7 @@ def tile_picked_ymatch_sum_p_kernel(tc, x_words, x_scales, w1, e_words, e_scales
         x_scale_picked = held.tile([P, S], U8, name="x_scale_picked", align_bytes=64)
         e_scale_picked = held.tile([P, U], U8, name="e_scale_picked", tag="e_scale_picked_then_h_scale", align_bytes=64)
         x_codes = [held.tile([P, S], U32, name=f"x_codes{g}", align_bytes=64) for g in range(PASSES)]
-        e_codes = [held.tile([P, U // 2], U32, name=f"e_codes{u}", align_bytes=64) for u in range(2)]
+        e_codes = held.tile([P, U], U32, name="e_codes", align_bytes=64)
         h_ps = [psum.tile([P, PACK, Q_TILE], F32, name=f"h_ps{b}") for b in range(Q_TILES)]
         y_ps = [psum.tile([P, U], F32, name=f"y_ps{b}") for b in range(Q_TILES)]
         h_bf = held.tile([P, Q_TILES, Q_TILE, PACK], BF16, name="h_bf", align_bytes=64)
@@ -139,23 +140,22 @@ def tile_picked_ymatch_sum_p_kernel(tc, x_words, x_scales, w1, e_words, e_scales
 
         h_scale_first = held.tile([P, Q_TILE], U8, name="h_scale_first", align_bytes=64)
         quantise_h(h_scale_first, 0, 1)
-        for u in range(2):
-            cols = slice(u * U // 2 // LIST_ROWS, (u + 1) * U // 2 // LIST_ROWS)
-            nc.vector.tensor_copy(e_codes[u][:], e_table[:].bitcast(U32).indirect(sup_sb[:, cols]))
+        for lo, hi in ((0, U - LAST_SUPPORTS), (U - LAST_SUPPORTS, U)):
+            nc.vector.tensor_copy(e_codes[:, lo:hi], e_table[:].bitcast(U32).indirect(sup_sb[:, lo // LIST_ROWS : hi // LIST_ROWS]))
         h_scale = held.tile([P, S], U8, name="h_scale", tag="e_scale_picked_then_h_scale", align_bytes=64)
         quantise_h(h_scale, 1, 2)
         quantise_h(h_scale, 2, Q_TILES)
 
         for b in range(Q_TILES):
             cols = slice(b * Q_TILE, (b + 1) * Q_TILE)
-            for u in range(2):
-                half = slice(u * U // 2, (u + 1) * U // 2)
+            edges = (0, U // 2, U - LAST_SUPPORTS, U) if b == 0 else (0, U)
+            for lo, hi in zip(edges, edges[1:]):
                 nc.tensor.matmul_mx(
-                    out=y_ps[b][:, half],
+                    out=y_ps[b][:, lo:hi],
                     lhsT=h_codes[:, cols].bitcast(FP8X4),
                     lhsT_scale=(h_scale_first if b == 0 else h_scale)[:, cols],
-                    rhs=e_codes[u][:].bitcast(FP8X4),
-                    rhs_scale=e_scale[:, half],
+                    rhs=e_codes[:, lo:hi].bitcast(FP8X4),
+                    rhs_scale=e_scale[:, lo:hi],
                     start=True,
                     stop=True,
                 )
@@ -211,4 +211,4 @@ def tile_picked_ymatch_sum_p_kernel(tc, x_words, x_scales, w1, e_words, e_scales
             nc.vector.tensor_tensor(out=pair[3][:, cols], in0=ex[3][:, 0, cols], in1=ex[3][:, 1, cols], op=ALU.add)
         for cols in halves:
             nc.vector.tensor_scalar(out=prob[3][:, cols], in0=pair[3][:, cols], scalar1=inv[:, 3:4], scalar2=None, op0=ALU.mult)
-            nc.sync.dma_start(out=out[3 * Q_TILE :, cols], in_=prob[3][:, cols])
+        store(3)

@@ -205,10 +205,7 @@ def tile_picked_ymatch_sum_p_kernel(tc, x_words, x_scales, w1, e_words, e_scales
         for b in (1, 2):
             scale_rows_on_scalar(b)
             store(b)
+        add_pairs(nc.vector, 3)
         invert(3, 4)
-        halves = [slice(u * CLASSES // 2, (u + 1) * CLASSES // 2) for u in range(2)]
-        for cols in halves:
-            nc.vector.tensor_tensor(out=pair[3][:, cols], in0=ex[3][:, 0, cols], in1=ex[3][:, 1, cols], op=ALU.add)
-        for cols in halves:
-            nc.vector.tensor_scalar(out=prob[3][:, cols], in0=pair[3][:, cols], scalar1=inv[:, 3:4], scalar2=None, op0=ALU.mult)
+        scale_rows(nc.vector, 3)
         store(3)

@@ -193,18 +193,20 @@ def tile_picked_ymatch_sum_p_kernel(tc, x_words, x_scales, w1, e_words, e_scales
         def scale_rows_on_scalar(b):
             nc.scalar.activation(out=prob[b][:], in_=pair[b][:], func=ACT.Copy, scale=inv[:, b : b + 1])
 
-        for b in range(Q_TILES):
+        for b in range(Q_TILES - 1):
             row_max(b)
+        invert(0, 1)
+        row_max(Q_TILES - 1)
         add_pairs(nc.gpsimd, 0)
-        invert(0, 2)
-        add_pairs(nc.vector, 1)
         scale_rows(nc.vector, 0)
         store(0)
-        invert(2, 3)
+        add_pairs(nc.vector, 1)
+        invert(1, 3)
         add_pairs(nc.vector, 2)
-        for b in (1, 2):
-            scale_rows_on_scalar(b)
-            store(b)
+        scale_rows(nc.vector, 1)
+        store(1)
+        scale_rows_on_scalar(2)
+        store(2)
         add_pairs(nc.vector, 3)
         invert(3, 4)
         scale_rows(nc.vector, 3)

@@ -143,8 +143,8 @@ def tile_picked_ymatch_sum_p_kernel(tc, x_words, x_scales, w1, e_words, e_scales
         for lo, hi in ((0, U - LAST_SUPPORTS), (U - LAST_SUPPORTS, U)):
             nc.vector.tensor_copy(e_codes[:, lo:hi], e_table[:].bitcast(U32).indirect(sup_sb[:, lo // LIST_ROWS : hi // LIST_ROWS]))
         h_scale = held.tile([P, S], U8, name="h_scale", tag="e_scale_picked_then_h_scale", align_bytes=64)
-        quantise_h(h_scale, 1, 2)
-        quantise_h(h_scale, 2, Q_TILES)
+        quantise_h(h_scale, 1, 3)
+        quantise_h(h_scale, 3, Q_TILES)
 
         for b in range(Q_TILES):
             cols = slice(b * Q_TILE, (b + 1) * Q_TILE)

@@ -40,8 +40,8 @@ def tile_picked_ymatch_sum_p_kernel(tc, x_words, x_scales, w1, e_words, e_scales
         offs_sb = lists.tile([P, S // LIST_ROWS], U16, name="offs_sb")
         sup_sb = lists.tile([P, U // LIST_ROWS], U16, name="sup_sb")
 
-        x_scale_table = held.tile([P, T], U8, name="x_scale_table", align_bytes=64)
-        e_scale_table = held.tile([P, W], U8, name="e_scale_table", align_bytes=64)
+        x_scale_table = held.tile([P, T], U8, name="x_scale_table", align_bytes=256)
+        e_scale_table = held.tile([P, W], U8, name="e_scale_table", align_bytes=256)
         x_scale = held.tile([P, PASSES * S], U8, name="x_scale", align_bytes=64)
         e_scale = held.tile([P, U], U8, name="e_scale", align_bytes=64)
         nc.vector.memset(e_scale_table[:].bitcast(I32), 0)
@@ -50,9 +50,9 @@ def tile_picked_ymatch_sum_p_kernel(tc, x_words, x_scales, w1, e_words, e_scales
         nc.vector.memset(x_scale[:].bitcast(I32), 0)
         nc.vector.memset(e_scale[:].bitcast(I32), 0)
 
-        w_raw = [held.tile([P, PACK, H], F32, name=f"w_raw{g}") for g in range(PASSES)]
-        x_table = [held.tile([P, T], I32, name=f"x_table{g}", align_bytes=64) for g in range(PASSES)]
-        e_table = held.tile([P, W], I32, name="e_table", align_bytes=64)
+        w_raw = [held.tile([P, PACK, H], F32, name=f"w_raw{g}", align_bytes=256) for g in range(PASSES)]
+        x_table = [held.tile([P, T], I32, name=f"x_table{g}", align_bytes=256) for g in range(PASSES)]
+        e_table = held.tile([P, W], I32, name="e_table", align_bytes=256)
         w_bf = [held.tile([P, PACK, P, PACK], BF16, name=f"w_bf{g}", align_bytes=64) for g in range(PASSES)]
         w_codes = [held.tile([P, H], U32, name=f"w_codes{g}", align_bytes=64) for g in range(PASSES)]
         w_scale = [held.tile([P, H], U8, name=f"w_scale{g}", align_bytes=64) for g in range(PASSES)]
@@ -165,7 +165,7 @@ def tile_picked_ymatch_sum_p_kernel(tc, x_words, x_scales, w1, e_words, e_scales
         inv = held.tile([P, Q_TILES], F32, name="inv")
         ex = [held.tile([P, D, CLASSES], F32, name=f"ex{b}") for b in range(Q_TILES)]
         pair = [held.tile([P, CLASSES], F32, name=f"pair{b}") for b in range(Q_TILES)]
-        prob = [held.tile([P, CLASSES], F32, name=f"prob{b}") for b in range(Q_TILES)]
+        prob = [held.tile([P, CLASSES], F32, name=f"prob{b}", align_bytes=256) for b in range(Q_TILES)]
 
         def row_max(b):
             nc.vector.tensor_reduce(out=neg_max[b][:], in_=y_ps[b][:], axis=mybir.AxisListType.X, op=ALU.max, negate=True)

@@ -42,8 +42,8 @@ def tile_picked_ymatch_sum_p_kernel(tc, x_words, x_scales, w1, e_words, e_scales
 
         x_scale_table = held.tile([P, T], U8, name="x_scale_table", align_bytes=256)
         e_scale_table = held.tile([P, W], U8, name="e_scale_table", align_bytes=256)
-        x_scale = held.tile([P, PASSES * S], U8, name="x_scale", align_bytes=64)
-        e_scale = held.tile([P, U], U8, name="e_scale", align_bytes=64)
+        x_scale = held.tile([P, PASSES * S], U8, name="x_scale", align_bytes=256)
+        e_scale = held.tile([P, U], U8, name="e_scale", align_bytes=256)
         nc.vector.memset(e_scale_table[:].bitcast(I32), 0)
         nc.vector.memset(x_scale_table[32:64, :].bitcast(I32), 0)
         nc.vector.memset(x_scale_table[64:P, :].bitcast(I32), 0)
@@ -53,17 +53,17 @@ def tile_picked_ymatch_sum_p_kernel(tc, x_words, x_scales, w1, e_words, e_scales
         w_raw = [held.tile([P, PACK, H], F32, name=f"w_raw{g}", align_bytes=256) for g in range(PASSES)]
         x_table = [held.tile([P, T], I32, name=f"x_table{g}", align_bytes=256) for g in range(PASSES)]
         e_table = held.tile([P, W], I32, name="e_table", align_bytes=256)
-        w_bf = [held.tile([P, PACK, P, PACK], BF16, name=f"w_bf{g}", align_bytes=64) for g in range(PASSES)]
-        w_codes = [held.tile([P, H], U32, name=f"w_codes{g}", align_bytes=64) for g in range(PASSES)]
-        w_scale = [held.tile([P, H], U8, name=f"w_scale{g}", align_bytes=64) for g in range(PASSES)]
-        x_scale_picked = held.tile([P, S], U8, name="x_scale_picked", align_bytes=64)
-        e_scale_picked = held.tile([P, U], U8, name="e_scale_picked", tag="e_scale_picked_then_h_scale", align_bytes=64)
-        x_codes = [held.tile([P, S], U32, name=f"x_codes{g}", align_bytes=64) for g in range(PASSES)]
-        e_codes = held.tile([P, U], U32, name="e_codes", align_bytes=64)
+        w_bf = [held.tile([P, PACK, P, PACK], BF16, name=f"w_bf{g}", align_bytes=256) for g in range(PASSES)]
+        w_codes = [held.tile([P, H], U32, name=f"w_codes{g}", align_bytes=256) for g in range(PASSES)]
+        w_scale = [held.tile([P, H], U8, name=f"w_scale{g}", align_bytes=256) for g in range(PASSES)]
+        x_scale_picked = held.tile([P, S], U8, name="x_scale_picked", align_bytes=256)
+        e_scale_picked = held.tile([P, U], U8, name="e_scale_picked", tag="e_scale_picked_then_h_scale", align_bytes=256)
+        x_codes = [held.tile([P, S], U32, name=f"x_codes{g}", align_bytes=256) for g in range(PASSES)]
+        e_codes = held.tile([P, U], U32, name="e_codes", align_bytes=256)
         h_ps = [psum.tile([P, PACK, Q_TILE], F32, name=f"h_ps{b}") for b in range(Q_TILES)]
         y_ps = [psum.tile([P, U], F32, name=f"y_ps{b}") for b in range(Q_TILES)]
-        h_bf = held.tile([P, Q_TILES, Q_TILE, PACK], BF16, name="h_bf", align_bytes=64)
-        h_codes = held.tile([P, S], U32, name="h_codes", align_bytes=64)
+        h_bf = held.tile([P, Q_TILES, Q_TILE, PACK], BF16, name="h_bf", align_bytes=256)
+        h_codes = held.tile([P, S], U32, name="h_codes", align_bytes=256)
 
         def load_w(g):
             nc.sync.dma_start(out=w_raw[g][:], in_=w1[g * K_PASS : (g + 1) * K_PASS, :].rearrange("(p j) c -> p j c", j=PACK))
@@ -138,11 +138,11 @@ def tile_picked_ymatch_sum_p_kernel(tc, x_words, x_scales, w1, e_words, e_scales
                 out=h_codes[:, cols].bitcast(FP8X4), scales=scale[:, cols], in_=h_bf[:, lo:hi].rearrange("p b q t -> p (b q t)")
             )
 
-        h_scale_first = held.tile([P, Q_TILE], U8, name="h_scale_first", align_bytes=64)
+        h_scale_first = held.tile([P, Q_TILE], U8, name="h_scale_first", align_bytes=256)
         quantise_h(h_scale_first, 0, 1)
         for lo, hi in ((0, U - LAST_SUPPORTS), (U - LAST_SUPPORTS, U)):
             nc.vector.tensor_copy(e_codes[:, lo:hi], e_table[:].bitcast(U32).indirect(sup_sb[:, lo // LIST_ROWS : hi // LIST_ROWS]))
-        h_scale = held.tile([P, S], U8, name="h_scale", tag="e_scale_picked_then_h_scale", align_bytes=64)
+        h_scale = held.tile([P, S], U8, name="h_scale", tag="e_scale_picked_then_h_scale", align_bytes=256)
         quantise_h(h_scale, 1, 3)
         quantise_h(h_scale, 3, Q_TILES)
 
@@ -163,8 +163,8 @@ def tile_picked_ymatch_sum_p_kernel(tc, x_words, x_scales, w1, e_words, e_scales
         neg_max = [held.tile([P, 1], F32, name=f"neg_max{b}") for b in range(Q_TILES)]
         total = held.tile([P, Q_TILES], F32, name="total")
         inv = held.tile([P, Q_TILES], F32, name="inv")
-        ex = [held.tile([P, D, CLASSES], F32, name=f"ex{b}") for b in range(Q_TILES)]
-        pair = [held.tile([P, CLASSES], F32, name=f"pair{b}") for b in range(Q_TILES)]
+        ex = [held.tile([P, D, CLASSES], F32, name=f"ex{b}", align_bytes=256) for b in range(Q_TILES)]
+        pair = [held.tile([P, CLASSES], F32, name=f"pair{b}", align_bytes=256) for b in range(Q_TILES)]
         prob = [held.tile([P, CLASSES], F32, name=f"prob{b}", align_bytes=256) for b in range(Q_TILES)]
 
         def row_max(b):

@@ -66,10 +66,10 @@ def tile_picked_ymatch_sum_p_kernel(tc, x_words, x_scales, w1, e_words, e_scales
         h_codes = held.tile([P, S], U32, name="h_codes", align_bytes=256)
 
         def load_w(g):
-            nc.sync.dma_start(out=w_raw[g][:], in_=w1[g * K_PASS : (g + 1) * K_PASS, :].rearrange("(p j) c -> p j c", j=PACK))
+            nc.sync.dma_start(out=w_raw[g][:], in_=w1[g * K_PASS : (g + 1) * K_PASS, :].rearrange("(p j) c -> p j c", j=PACK), max_dma_last_dim=4096)
 
         def load_words(table, words):
-            nc.sync.dma_start(out=table[:], in_=words.rearrange("p n j -> p (n j)").bitcast(I32))
+            nc.sync.dma_start(out=table[:], in_=words.rearrange("p n j -> p (n j)").bitcast(I32), max_dma_last_dim=4096)
 
         def round_w(g):
             rounded = w_bf[g][:].rearrange("p t m j -> p m t j")

from contextlib import ExitStack

import concourse.mybir as mybir

K, T, S, H, D, W, U = 1024, 2048, 512, 512, 2, 2048, 512
FLOPS = 2 * K * H * S + 2 * H * S * U

F32 = mybir.dt.float32
BF16 = mybir.dt.bfloat16
I32 = mybir.dt.int32
U32 = mybir.dt.uint32
U16 = mybir.dt.uint16
U8 = mybir.dt.uint8
FP8X4 = mybir.dt.float8_e4m3fn_x4
ALU = mybir.AluOpType
ACT = mybir.ActivationFunctionType

P = 128
PACK = 4
K_PASS = P * PACK
PASSES = K // K_PASS
QUADS = 4
QUAD_ROWS = 4
LIST_ROWS = 16
Q_TILE = 128
Q_TILES = S // Q_TILE
GATHER_TILES = ((4,), (1, 1, 2))
LAST_SUPPORTS = 128
CLASSES = U // D
SCALAR_GROUPS = 44


def tile_picked_ymatch_sum_p_kernel(tc, x_words, x_scales, w1, e_words, e_scales, offs, sup, out):
    nc = tc.nc
    with ExitStack() as ctx:
        lists = ctx.enter_context(tc.tile_pool(name="lists", bufs=1))
        held = ctx.enter_context(tc.tile_pool(name="held", bufs=1))
        psum = ctx.enter_context(tc.psum_pool(name="psum", bufs=1))

        offs_sb = lists.tile([P, S // LIST_ROWS], U16, name="offs_sb")
        sup_sb = lists.tile([P, U // LIST_ROWS], U16, name="sup_sb")

        x_scale_table = held.tile([P, T], U8, name="x_scale_table", align_bytes=256)
        e_scale_table = held.tile([P, W], U8, name="e_scale_table", align_bytes=256)
        x_scale = held.tile([P, PASSES * S], U8, name="x_scale", align_bytes=256)
        e_scale = held.tile([P, U], U8, name="e_scale", align_bytes=256)
        nc.vector.memset(e_scale_table[:].bitcast(I32), 0)
        nc.vector.memset(x_scale_table[32:64, :].bitcast(I32), 0)
        nc.vector.memset(x_scale_table[64:P, :].bitcast(I32), 0)
        nc.vector.memset(x_scale[:].bitcast(I32), 0)
        nc.vector.memset(e_scale[:].bitcast(I32), 0)

        w_raw = [held.tile([P, PACK, H], F32, name=f"w_raw{g}", align_bytes=256) for g in range(PASSES)]
        x_table = [held.tile([P, T], I32, name=f"x_table{g}", align_bytes=256) for g in range(PASSES)]
        e_table = held.tile([P, W], I32, name="e_table", align_bytes=256)
        w_bf = [held.tile([P, PACK, P, PACK], BF16, name=f"w_bf{g}", align_bytes=256) for g in range(PASSES)]
        w_codes = [held.tile([P, H], U32, name=f"w_codes{g}", align_bytes=256) for g in range(PASSES)]
        w_scale = [held.tile([P, H], U8, name=f"w_scale{g}", align_bytes=256) for g in range(PASSES)]
        x_scale_picked = held.tile([P, S], U8, name="x_scale_picked", align_bytes=256)
        e_scale_picked = held.tile([P, U], U8, name="e_scale_picked", tag="e_scale_picked_then_h_scale", align_bytes=256)
        x_codes = [held.tile([P, S], U32, name=f"x_codes{g}", align_bytes=256) for g in range(PASSES)]
        e_codes = held.tile([P, U], U32, name="e_codes", align_bytes=256)
        h_ps = [psum.tile([P, PACK, Q_TILE], F32, name=f"h_ps{b}") for b in range(Q_TILES)]
        y_ps = [psum.tile([P, U], F32, name=f"y_ps{b}") for b in range(Q_TILES)]
        h_bf = held.tile([P, Q_TILES, Q_TILE, PACK], BF16, name="h_bf", align_bytes=256)
        h_codes = held.tile([P, S], U32, name="h_codes", align_bytes=256)

        def load_w(g):
            nc.sync.dma_start(out=w_raw[g][:], in_=w1[g * K_PASS : (g + 1) * K_PASS, :].rearrange("(p j) c -> p j c", j=PACK), max_dma_last_dim=4096)

        def load_words(table, words):
            nc.sync.dma_start(out=table[:], in_=words.rearrange("p n j -> p (n j)").bitcast(I32), max_dma_last_dim=4096)

        def round_w(g):
            rounded = w_bf[g][:].rearrange("p t m j -> p m t j")
            raw = w_raw[g][:].rearrange("p j (m t) -> p m t j", t=PACK)
            nc.scalar.copy(out=rounded[:, :SCALAR_GROUPS], in_=raw[:, :SCALAR_GROUPS])
            nc.vector.tensor_copy(out=rounded[:, SCALAR_GROUPS:], in_=raw[:, SCALAR_GROUPS:])

        def quantise_w(g):
            nc.vector.quantize_mx(out=w_codes[g][:].bitcast(FP8X4), scales=w_scale[g][:], in_=w_bf[g][:].rearrange("p t m j -> p (t m j)"))

        def gather_x(g):
            lo = 0
            for tiles in GATHER_TILES[g]:
                hi = lo + tiles * Q_TILE
                picked = x_table[g][:].bitcast(U32).indirect(offs_sb[:, lo // LIST_ROWS : hi // LIST_ROWS])
                nc.vector.tensor_copy(x_codes[g][:, lo:hi], picked)
                lo = hi

        def project(g):
            for b in range(Q_TILES):
                for t in range(PACK):
                    nc.tensor.matmul_mx(
                        out=h_ps[b][:, t, :],
                        lhsT=w_codes[g][:, t * P : (t + 1) * P].bitcast(FP8X4),
                        lhsT_scale=w_scale[g][:, t * P : (t + 1) * P],
                        rhs=x_codes[g][:, b * Q_TILE : (b + 1) * Q_TILE].bitcast(FP8X4),
                        rhs_scale=x_scale[:, g * S + b * Q_TILE : g * S + (b + 1) * Q_TILE],
                        start=(g == 0 and t == 0),
                        stop=(g == PASSES - 1 and t == PACK - 1),
                    )

        nc.sync.dma_start(out=x_scale_table[0:32, :].bitcast(I32), in_=x_scales.rearrange("g j c -> j g c").bitcast(I32))
        nc.sync.dma_start(offs_sb[:], offs)
        load_words(x_table[0], x_words[0])
        nc.sync.dma_start(sup_sb[:], sup)
        nc.sync.dma_start(out=e_scale_table[0:P:8, :].bitcast(I32), in_=e_scales[0].bitcast(I32))
        load_w(0)

        nc.vector.tensor_copy(x_scale_picked[:], x_scale_table[:].indirect(offs_sb[:]))
        for q in range(QUADS):
            nc.sync.dma_start(
                out=x_scale[32 * q : 32 * q + QUAD_ROWS, :].bitcast(I32), in_=x_scale_picked[8 * q : 8 * q + 8, :].bitcast(I32)
            )
        load_w(1)
        load_words(x_table[1], x_words[1])
        load_words(e_table, e_words[0])
        gather_x(0)
        nc.vector.tensor_copy(e_scale_picked[:], e_scale_table[:].indirect(sup_sb[:]))
        for r in range(QUAD_ROWS):
            nc.sync.dma_start(out=e_scale[r:P:32, :].bitcast(I32), in_=e_scale_picked[8 * r : P : 32, :].bitcast(I32))

        round_w(0)
        quantise_w(0)
        project(0)
        round_w(1)
        quantise_w(1)
        gather_x(1)
        project(1)

        for b in range(Q_TILES):
            nc.scalar.copy(out=h_bf[:, b], in_=h_ps[b][:].rearrange("p t q -> p q t"))

        def quantise_h(scale, lo, hi):
            cols = slice(lo * Q_TILE, hi * Q_TILE)
            nc.vector.quantize_mx(
                out=h_codes[:, cols].bitcast(FP8X4), scales=scale[:, cols], in_=h_bf[:, lo:hi].rearrange("p b q t -> p (b q t)")
            )

        h_scale_first = held.tile([P, Q_TILE], U8, name="h_scale_first", align_bytes=256)
        quantise_h(h_scale_first, 0, 1)
        for lo, hi in ((0, U - LAST_SUPPORTS), (U - LAST_SUPPORTS, U)):
            nc.vector.tensor_copy(e_codes[:, lo:hi], e_table[:].bitcast(U32).indirect(sup_sb[:, lo // LIST_ROWS : hi // LIST_ROWS]))
        h_scale = held.tile([P, S], U8, name="h_scale", tag="e_scale_picked_then_h_scale", align_bytes=256)
        quantise_h(h_scale, 1, 3)
        quantise_h(h_scale, 3, Q_TILES)

        for b in range(Q_TILES):
            cols = slice(b * Q_TILE, (b + 1) * Q_TILE)
            edges = (0, U // 2, U - LAST_SUPPORTS, U) if b == 0 else (0, U)
            for lo, hi in zip(edges, edges[1:]):
                nc.tensor.matmul_mx(
                    out=y_ps[b][:, lo:hi],
                    lhsT=h_codes[:, cols].bitcast(FP8X4),
                    lhsT_scale=(h_scale_first if b == 0 else h_scale)[:, cols],
                    rhs=e_codes[:, lo:hi].bitcast(FP8X4),
                    rhs_scale=e_scale[:, lo:hi],
                    start=True,
                    stop=True,
                )

        neg_max = [held.tile([P, 1], F32, name=f"neg_max{b}") for b in range(Q_TILES)]
        total = held.tile([P, Q_TILES], F32, name="total")
        inv = held.tile([P, Q_TILES], F32, name="inv")
        ex = [held.tile([P, D, CLASSES], F32, name=f"ex{b}", align_bytes=256) for b in range(Q_TILES)]
        pair = [held.tile([P, CLASSES], F32, name=f"pair{b}", align_bytes=256) for b in range(Q_TILES)]
        prob = [held.tile([P, CLASSES], F32, name=f"prob{b}", align_bytes=256) for b in range(Q_TILES)]

        def row_max(b):
            nc.vector.tensor_reduce(out=neg_max[b][:], in_=y_ps[b][:], axis=mybir.AxisListType.X, op=ALU.max, negate=True)
            nc.scalar.activation(
                out=ex[b][:],
                in_=y_ps[b][:].rearrange("p (v d) -> p d v", d=D),
                func=ACT.Exp,
                bias=neg_max[b][:],
                scale=1.0,
                accum_out=total[:, b : b + 1],
            )

        def invert(lo, hi):
            nc.vector.reciprocal(out=inv[:, lo:hi], in_=total[:, lo:hi])

        def add_pairs(engine, b):
            engine.tensor_tensor(out=pair[b][:], in0=ex[b][:, 0, :], in1=ex[b][:, 1, :], op=ALU.add)

        def scale_rows(engine, b):
            engine.tensor_scalar(out=prob[b][:], in0=pair[b][:], scalar1=inv[:, b : b + 1], scalar2=None, op0=ALU.mult)

        def store(b):
            nc.sync.dma_start(out=out[b * Q_TILE : (b + 1) * Q_TILE, :], in_=prob[b][:])

        def scale_rows_on_scalar(b):
            nc.scalar.activation(out=prob[b][:], in_=pair[b][:], func=ACT.Copy, scale=inv[:, b : b + 1])

        for b in range(Q_TILES - 1):
            row_max(b)
        invert(0, 1)
        row_max(Q_TILES - 1)
        add_pairs(nc.gpsimd, 0)
        scale_rows(nc.vector, 0)
        store(0)
        add_pairs(nc.vector, 1)
        invert(1, 3)
        add_pairs(nc.vector, 2)
        scale_rows(nc.vector, 1)
        store(1)
        scale_rows_on_scalar(2)
        store(2)
        add_pairs(nc.vector, 3)
        invert(3, 4)
        scale_rows(nc.vector, 3)
        store(3)
